import numpy as np
import ml_dtypes


def mxq(x, axis, fmt="e4m3"):
    dtype, down = {"e4m3": (ml_dtypes.float8_e4m3fn, 7), "e5m2": (ml_dtypes.float8_e5m2, 14)}[fmt]
    v = np.moveaxis(np.asarray(x, np.float32).astype(ml_dtypes.bfloat16).astype(np.float64), axis, -1)
    blocks = v.reshape(v.shape[:-1] + (-1, 32))
    amax = np.abs(blocks).max(-1, keepdims=True)
    byte = np.maximum(np.where(amax > 0, np.frexp(amax)[1] - 1 + 127, 0) - down, 1)
    scale = np.exp2(byte - 127.0)
    codes = (blocks / scale).astype(np.float32).astype(dtype).astype(np.float64)
    return np.moveaxis((codes * scale).reshape(v.shape), -1, axis)


WIDE = False


def mx_kscale(k):
    if not WIDE:
        return np.ones(k)
    levels = np.array([10, -10, 5, -5, 0])
    if k % 512:
        return np.exp2(np.random.permutation(np.resize(levels, k // 32))).repeat(32)
    a = np.empty((k // 512, 16))
    for p in range(k // 512):
        a[p, :8] = np.random.permutation(np.resize(levels, 8))
        for g in range(8):
            far = levels[np.abs(levels - a[p, g]) >= 10]
            a[p, g + 8] = far[np.random.randint(len(far))]
    return np.exp2(a.ravel()).repeat(32)


def f64(x):
    return np.asarray(x).astype(np.float64)


def striped8(idx):
    return np.concatenate([x.reshape(-1, 16).T for x in idx]).astype(np.uint16)


def runs(offs, k):
    lists = np.stack([offs[16 * r : 16 * r + 16].T.reshape(-1) for r in range(8)]).astype(np.int64)
    return lists[np.arange(k) % 512 // 64]


def pack_weight(w):
    k, n = w.shape
    w = f64(np.asarray(w, np.float32).astype(ml_dtypes.bfloat16)).reshape(k // 32, 32, n)
    amax = np.abs(w).max(1)
    byte = np.clip(np.where(amax > 0, np.frexp(amax)[1] - 1 + 127 - 7, 1), 1, 254)
    scaled = (w * np.exp2(127.0 - byte)[:, None, :]).reshape(k, n).astype(np.float32)
    words = np.ascontiguousarray(scaled.reshape(k // 512, 128, 4, n).transpose(0, 1, 3, 2)).astype(ml_dtypes.float8_e4m3fn).view(np.uint8)
    return words, np.ascontiguousarray(byte.astype(np.uint8).reshape(k // 512, 16, n))


def unpack_weight(words, scales):
    g, p, n, _ = words.shape
    vals = np.ascontiguousarray(words).view(ml_dtypes.float8_e4m3fn).astype(np.float64) * np.repeat(np.exp2(scales.astype(np.float64) - 127.0), 8, axis=1)[..., None]
    return vals.transpose(0, 1, 3, 2).reshape(g * 512, n)


def sigmoid(v):
    return 1.0 / (1.0 + np.exp(-np.maximum(v, -700.0)))

def planes(y):
    n, m = y.shape
    v = y.astype(np.float32).astype(ml_dtypes.bfloat16).astype(np.float64).reshape(n // 32, 32, m)
    top = np.abs(v).max(1)
    byte = np.clip(np.where(top > 0, np.frexp(top)[1] - 1 + 127 - 7, 1), 1, 254)
    codes = (v * np.exp2(127.0 - byte)[:, None, :]).reshape(n, m).astype(np.float32).astype(ml_dtypes.float8_e4m3fn).view(np.uint8)
    words = codes.reshape(n // 512, 128, 4, m).transpose(0, 1, 3, 2)
    return np.ascontiguousarray(words), np.ascontiguousarray(byte.astype(np.uint8).reshape(n // 512, 16, m))


K, T, S, N = 512, 2048, 512, 512


def setup_inputs():
    n = np.random.standard_normal
    s = mx_kscale(K)[:, None]
    packed_xT = pack_weight(n((K, T)) * s)
    return {
        "x_words": packed_xT[0],
        "x_scales": packed_xT[1],
        "w1": (n((K, N)) / np.sqrt(K) / s).astype(np.float32),
        "w2": (n((K, N)) / np.sqrt(K) / s).astype(np.float32),
        "st": n((N, S)).astype(np.float32),
        "offs": striped8(np.stack([np.random.permutation(T)[:S] for _ in range(8)])),
    }


def reference(x_words, x_scales, w1, w2, st, offs):
    xq = unpack_weight(x_words, x_scales)[np.arange(K)[:, None], runs(offs, K)]
    f = sigmoid(mxq(f64(w1), 0, "e4m3").T @ xq)
    g = np.tanh(mxq(f64(w2), 0, "e4m3").T @ xq)
    out_0 = f64(st) + f * (g - f64(st))
    return (out_0,) + planes(out_0)

@@ -1,0 +1,151 @@
+from contextlib import ExitStack
+
+import concourse.mybir as mybir
+
+K, T, S, N = 512, 2048, 512, 512
+FLOPS = 2 * 2 * K * N * S
+
+F32 = mybir.dt.float32
+BF16 = mybir.dt.bfloat16
+I32 = mybir.dt.int32
+U32 = mybir.dt.uint32
+U16 = mybir.dt.uint16
+U8 = mybir.dt.uint8
+FP8X4 = mybir.dt.float8_e4m3fn_x4
+ACT = mybir.ActivationFunctionType
+ALU = mybir.AluOpType
+
+P = 128
+PACK = 4
+HALF = N // 2
+CHUNK = 128
+CHUNKS = S // CHUNK
+
+
+def tile_picked_phcell_none_po_kernel(tc, x_words, x_scales, w1, w2, st, offs, out_0, out_1, out_2):
+    nc = tc.nc
+    with ExitStack() as ctx:
+        keep = ctx.enter_context(tc.tile_pool(name="keep", bufs=1))
+        psum = ctx.enter_context(tc.psum_pool(name="psum", bufs=1))
+
+        offsets = keep.tile([P, S // 16], U16, name="offsets")
+        nc.sync.dma_start(offsets[:], offs)
+
+        scale_table = keep.tile([P, T], U8, name="scale_table", align_bytes=64)
+        nc.vector.memset(scale_table[:].bitcast(I32), 0)
+        nc.scalar.dma_start(out=scale_table[0:P:8, :].bitcast(I32), in_=x_scales[0].bitcast(I32))
+        x_scale = keep.tile([P, S], U8, name="x_scale", align_bytes=64)
+        nc.vector.memset(x_scale[:].bitcast(I32), 0)
+
+        word_table = keep.tile([P, T], U32, name="word_table", align_bytes=64)
+        nc.sync.dma_start(out=word_table[:].bitcast(I32), in_=x_words[0].rearrange("p c r -> p (c r)").bitcast(I32))
+
+        def load_weight(w, name):
+            halves = []
+            for h in range(2):
+                raw = keep.tile([P, PACK, HALF], F32, name=f"{name}_raw{h}")
+                nc.sync.dma_start(out=raw[:], in_=w.rearrange("(p j) c -> p j c", j=PACK)[:, :, h * HALF : (h + 1) * HALF])
+                halves.append(raw)
+            return halves
+
+        w2_raw = load_weight(w2, "w2")
+        w1_raw = load_weight(w1, "w1")
+
+        picked_scales = keep.tile([P, S], U8, name="picked_scales", tag="late", align_bytes=64)
+        nc.vector.tensor_copy(picked_scales[:], scale_table[:].indirect(offsets[:]))
+        for i in range(4):
+            nc.scalar.dma_start(out=x_scale[i:P:32, :].bitcast(I32), in_=picked_scales[8 * i : P : 32, :].bitcast(I32))
+        x_codes = keep.tile([P, S], U32, name="x_codes", align_bytes=64)
+        nc.vector.tensor_copy(x_codes[:], word_table[:].indirect(offsets[:]))
+
+        state = keep.tile([P, PACK * S], F32, name="state", tag="late", align_bytes=64)
+        st_rows = st.rearrange("(p t) j -> p (t j)", t=PACK)
+        for h in range(2):
+            nc.sync.dma_start(out=state[:, 2 * S * h : 2 * S * (h + 1)], in_=st_rows[:, 2 * S * h : 2 * S * (h + 1)])
+        state_t = state[:].rearrange("p (t j) -> p t j", t=PACK)
+
+        def round_half(grouped, raw, h):
+            dst = grouped[:].rearrange("p (t m j) -> p m t j", t=PACK, j=PACK)[:, h * 64 : (h + 1) * 64]
+            src = raw[:].rearrange("p j (m t) -> p m t j", t=PACK)
+            if h == 0:
+                nc.scalar.activation(dst, src, ACT.Copy)
+            else:
+                nc.vector.tensor_copy(dst, src)
+
+        w2_bf = keep.tile([P, PACK * N], BF16, name="w2_bf", align_bytes=64)
+        w1_bf = keep.tile([P, PACK * N], BF16, name="w1_bf", align_bytes=64)
+        for h in range(2):
+            round_half(w2_bf, w2_raw[h], h)
+        w2_codes = keep.tile([P, N], U32, name="w2_codes", align_bytes=64)
+        w2_scale = keep.tile([P, N], U8, name="w2_scale", align_bytes=64)
+        for u in range(2):
+            nc.vector.quantize_mx(out=w2_codes[:, u * HALF : (u + 1) * HALF].bitcast(FP8X4), scales=w2_scale[:, u * HALF : (u + 1) * HALF], in_=w2_bf[:, u * 1024 : (u + 1) * 1024])
+        for h in range(2):
+            round_half(w1_bf, w1_raw[h], h)
+        new = []
+        for t in range(PACK):
+            cols = slice(t * P, (t + 1) * P)
+            bank = psum.tile([P, S], F32, name=f"new_bank{t}")
+            nc.tensor.matmul_mx(out=bank[:], lhsT=w2_codes[:, cols].bitcast(FP8X4), lhsT_scale=w2_scale[:, cols], rhs=x_codes[:].bitcast(FP8X4), rhs_scale=x_scale[:], start=True, stop=True)
+            g = keep.tile([P, S], F32, name=f"new{t}")
+            nc.scalar.activation(g[:], bank[:], ACT.Tanh)
+            new.append(g)
+        w1_codes = keep.tile([P, N], U32, name="w1_codes", align_bytes=64)
+        w1_scale = keep.tile([P, N], U8, name="w1_scale", align_bytes=64)
+        nc.vector.quantize_mx(out=w1_codes[:].bitcast(FP8X4), scales=w1_scale[:], in_=w1_bf[:])
+
+        diff = keep.tile([P, PACK, S], F32, name="diff")
+        for t in range(PACK):
+            nc.vector.tensor_tensor(diff[:, t, :], new[t][:], state_t[:, t, :], ALU.subtract)
+
+        gates = []
+        for q in range(CHUNKS):
+            places = slice(q * CHUNK, (q + 1) * CHUNK)
+            bank = psum.tile([P, PACK, CHUNK], F32, name=f"gate_bank{q}")
+            for t in range(PACK):
+                cols = slice(t * P, (t + 1) * P)
+                nc.tensor.matmul_mx(out=bank[:, t, :], lhsT=w1_codes[:, cols].bitcast(FP8X4), lhsT_scale=w1_scale[:, cols], rhs=x_codes[:, places].bitcast(FP8X4), rhs_scale=x_scale[:, places], start=True, stop=True)
+            gate = keep.tile([P, PACK, CHUNK], F32, name=f"gate{q}")
+            nc.scalar.activation(gate[:], bank[:], ACT.Tanh, scale=0.5)
+            gates.append(gate)
+
+        out_rows = out_0.rearrange("(p t) j -> p t j", t=PACK)
+        out_words = out_1[0].rearrange("p c r -> p (c r)").bitcast(I32)
+        y_scale = keep.tile([P, S], U8, name="y_scale", align_bytes=64)
+        y_codes = [keep.tile([P, 2 * CHUNK], U32, name=f"y_codes{u}", align_bytes=64) for u in range(2)]
+        step, y, y_bf = {}, {}, {}
+
+        def mul(q):
+            step[q] = keep.tile([P, PACK, CHUNK], F32, name=f"step{q}")
+            nc.vector.scalar_tensor_tensor(step[q][:], gates[q][:], 1.0, diff[:, :, q * CHUNK : (q + 1) * CHUNK], ALU.add, ALU.mult)
+
+        def add(q):
+            places = slice(q * CHUNK, (q + 1) * CHUNK)
+            y[q] = keep.tile([P, PACK, CHUNK], F32, name=f"y{q}")
+            nc.vector.scalar_tensor_tensor(y[q][:], step[q][:], 0.5, state_t[:, :, places], ALU.mult, ALU.add)
+            nc.sync.dma_start(out=out_rows[:, :, places], in_=y[q][:])
+            y_bf[q] = keep.tile([P, PACK * CHUNK], BF16, name=f"y_bf{q}", align_bytes=64)
+            dst = y_bf[q][:].rearrange("p (c i t) -> p c t i", i=4, t=PACK)
+            src = y[q][:].rearrange("p t (c i) -> p c t i", i=4)
+            if q < CHUNKS - 1:
+                nc.scalar.activation(dst, src, ACT.Copy)
+            else:
+                nc.vector.tensor_copy(dst, src)
+
+        def pack(q):
+            u, v = divmod(q, 2)
+            nc.vector.quantize_mx(out=y_codes[u][:, v * CHUNK : (v + 1) * CHUNK].bitcast(FP8X4), scales=y_scale[:, q * CHUNK : (q + 1) * CHUNK], in_=y_bf[q][:])
+            if v == 1:
+                nc.sync.dma_start(out=out_words[:, u * 2 * CHUNK : (u + 1) * 2 * CHUNK], in_=y_codes[u][:].bitcast(I32))
+
+        mul(0)
+        for q in range(CHUNKS):
+            if q + 1 < CHUNKS:
+                mul(q + 1)
+            add(q)
+            if q >= 1:
+                pack(q - 1)
+        pack(CHUNKS - 1)
+        for quad in range(4):
+            eng = nc.scalar if quad % 2 else nc.sync
+            eng.dma_start(out=out_2[0, 4 * quad : 4 * quad + 4, :].bitcast(I32), in_=y_scale[32 * quad : 32 * quad + 4, :].bitcast(I32))

@@ -18,6 +18,8 @@ ALU = mybir.AluOpType
 P = 128
 PACK = 4
 HALF = N // 2
+SCALAR_ROWS = 44
+LEAD = 768
 CHUNK = 128
 CHUNKS = S // CHUNK
 
@@ -28,75 +30,64 @@ def tile_picked_phcell_none_po_kernel(tc, x_words, x_scales, w1, w2, st, offs, o
         keep = ctx.enter_context(tc.tile_pool(name="keep", bufs=1))
         psum = ctx.enter_context(tc.psum_pool(name="psum", bufs=1))
 
+        scale_table = keep.tile([P, T], U8, name="scale_table", tag="late", align_bytes=64)
+        nc.vector.memset(scale_table[:].bitcast(I32), 0)
+        word_table = keep.tile([P, T], U32, name="word_table", tag="last", align_bytes=64)
+        words = x_words[0].rearrange("p c r -> p (c r)").bitcast(I32)
+        for cols in (slice(0, 512), slice(512, LEAD)):
+            nc.sync.dma_start(out=word_table[:, cols].bitcast(I32), in_=words[:, cols])
         offsets = keep.tile([P, S // 16], U16, name="offsets")
         nc.sync.dma_start(offsets[:], offs)
-
-        scale_table = keep.tile([P, T], U8, name="scale_table", align_bytes=64)
-        nc.vector.memset(scale_table[:].bitcast(I32), 0)
-        nc.scalar.dma_start(out=scale_table[0:P:8, :].bitcast(I32), in_=x_scales[0].bitcast(I32))
+        nc.sync.dma_start(out=scale_table[0:P:8, :].bitcast(I32), in_=x_scales[0].bitcast(I32))
+        nc.sync.dma_start(out=word_table[:, LEAD:].bitcast(I32), in_=words[:, LEAD:])
         x_scale = keep.tile([P, S], U8, name="x_scale", align_bytes=64)
         nc.vector.memset(x_scale[:].bitcast(I32), 0)
 
-        word_table = keep.tile([P, T], U32, name="word_table", align_bytes=64)
-        nc.sync.dma_start(out=word_table[:].bitcast(I32), in_=x_words[0].rearrange("p c r -> p (c r)").bitcast(I32))
+        w2_raw = keep.tile([P, PACK * N], F32, name="w2_raw")
+        nc.sync.dma_start(out=w2_raw[:], in_=w2.rearrange("(p j) c -> p (j c)", j=PACK))
 
-        def load_weight(w, name):
-            halves = []
-            for h in range(2):
-                raw = keep.tile([P, PACK, HALF], F32, name=f"{name}_raw{h}")
-                nc.sync.dma_start(out=raw[:], in_=w.rearrange("(p j) c -> p j c", j=PACK)[:, :, h * HALF : (h + 1) * HALF])
-                halves.append(raw)
-            return halves
-
-        w2_raw = load_weight(w2, "w2")
-        w1_raw = load_weight(w1, "w1")
-
-        picked_scales = keep.tile([P, S], U8, name="picked_scales", tag="late", align_bytes=64)
+        picked_scales = keep.tile([P, S], U8, name="picked_scales", align_bytes=64)
         nc.vector.tensor_copy(picked_scales[:], scale_table[:].indirect(offsets[:]))
         for i in range(4):
-            nc.scalar.dma_start(out=x_scale[i:P:32, :].bitcast(I32), in_=picked_scales[8 * i : P : 32, :].bitcast(I32))
+            nc.sync.dma_start(out=x_scale[i:P:32, :].bitcast(I32), in_=picked_scales[8 * i : P : 32, :].bitcast(I32))
         x_codes = keep.tile([P, S], U32, name="x_codes", align_bytes=64)
         nc.vector.tensor_copy(x_codes[:], word_table[:].indirect(offsets[:]))
 
-        state = keep.tile([P, PACK * S], F32, name="state", tag="late", align_bytes=64)
+        w1_raw = keep.tile([P, PACK * N], F32, name="w1_raw", tag="late", align_bytes=64)
+        nc.sync.dma_start(out=w1_raw[:], in_=w1.rearrange("(p j) c -> p (j c)", j=PACK))
+        state = keep.tile([P, PACK * S], F32, name="state", tag="last", align_bytes=64)
         st_rows = st.rearrange("(p t) j -> p (t j)", t=PACK)
         for h in range(2):
             nc.sync.dma_start(out=state[:, 2 * S * h : 2 * S * (h + 1)], in_=st_rows[:, 2 * S * h : 2 * S * (h + 1)])
         state_t = state[:].rearrange("p (t j) -> p t j", t=PACK)
 
-        def round_half(grouped, raw, h):
-            dst = grouped[:].rearrange("p (t m j) -> p m t j", t=PACK, j=PACK)[:, h * 64 : (h + 1) * 64]
-            src = raw[:].rearrange("p j (m t) -> p m t j", t=PACK)
-            if h == 0:
-                nc.scalar.activation(dst, src, ACT.Copy)
-            else:
-                nc.vector.tensor_copy(dst, src)
+        def round_weight(grouped, raw):
+            dst = grouped[:].rearrange("p (t m j) -> p m t j", t=PACK, j=PACK)
+            src = raw.rearrange("p (j m t) -> p m t j", j=PACK, t=PACK)
+            nc.scalar.activation(dst[:, :SCALAR_ROWS], src[:, :SCALAR_ROWS], ACT.Copy)
+            nc.vector.tensor_copy(dst[:, SCALAR_ROWS:], src[:, SCALAR_ROWS:])
 
         w2_bf = keep.tile([P, PACK * N], BF16, name="w2_bf", align_bytes=64)
         w1_bf = keep.tile([P, PACK * N], BF16, name="w1_bf", align_bytes=64)
-        for h in range(2):
-            round_half(w2_bf, w2_raw[h], h)
+        round_weight(w2_bf, w2_raw[:])
         w2_codes = keep.tile([P, N], U32, name="w2_codes", align_bytes=64)
         w2_scale = keep.tile([P, N], U8, name="w2_scale", align_bytes=64)
         for u in range(2):
             nc.vector.quantize_mx(out=w2_codes[:, u * HALF : (u + 1) * HALF].bitcast(FP8X4), scales=w2_scale[:, u * HALF : (u + 1) * HALF], in_=w2_bf[:, u * 1024 : (u + 1) * 1024])
-        for h in range(2):
-            round_half(w1_bf, w1_raw[h], h)
-        new = []
+        round_weight(w1_bf, w1_raw[:])
+        new = keep.tile([P, PACK, S], F32, name="new", tag="late", align_bytes=64)
         for t in range(PACK):
             cols = slice(t * P, (t + 1) * P)
             bank = psum.tile([P, S], F32, name=f"new_bank{t}")
             nc.tensor.matmul_mx(out=bank[:], lhsT=w2_codes[:, cols].bitcast(FP8X4), lhsT_scale=w2_scale[:, cols], rhs=x_codes[:].bitcast(FP8X4), rhs_scale=x_scale[:], start=True, stop=True)
-            g = keep.tile([P, S], F32, name=f"new{t}")
-            nc.scalar.activation(g[:], bank[:], ACT.Tanh)
-            new.append(g)
+            nc.scalar.activation(new[:, t, :], bank[:], ACT.Tanh)
         w1_codes = keep.tile([P, N], U32, name="w1_codes", align_bytes=64)
         w1_scale = keep.tile([P, N], U8, name="w1_scale", align_bytes=64)
         nc.vector.quantize_mx(out=w1_codes[:].bitcast(FP8X4), scales=w1_scale[:], in_=w1_bf[:])
 
         diff = keep.tile([P, PACK, S], F32, name="diff")
         for t in range(PACK):
-            nc.vector.tensor_tensor(diff[:, t, :], new[t][:], state_t[:, t, :], ALU.subtract)
+            nc.vector.tensor_tensor(diff[:, t, :], new[:, t, :], state_t[:, t, :], ALU.subtract)
 
         gates = []
         for q in range(CHUNKS):

@@ -86,8 +86,10 @@ def tile_picked_phcell_none_po_kernel(tc, x_words, x_scales, w1, w2, st, offs, o
         nc.vector.quantize_mx(out=w1_codes[:].bitcast(FP8X4), scales=w1_scale[:], in_=w1_bf[:])
 
         diff = keep.tile([P, PACK, S], F32, name="diff")
-        for t in range(PACK):
+        for t in range(PACK - 1):
             nc.vector.tensor_tensor(diff[:, t, :], new[:, t, :], state_t[:, t, :], ALU.subtract)
+        for places in (slice(0, S // 2), slice(S // 2, S)):
+            nc.vector.tensor_tensor(diff[:, PACK - 1, places], new[:, PACK - 1, places], state_t[:, PACK - 1, places], ALU.subtract)
 
         gates = []
         for q in range(CHUNKS):
@@ -104,39 +106,44 @@ def tile_picked_phcell_none_po_kernel(tc, x_words, x_scales, w1, w2, st, offs, o
         out_words = out_1[0].rearrange("p c r -> p (c r)").bitcast(I32)
         y_scale = keep.tile([P, S], U8, name="y_scale", align_bytes=64)
         y_codes = [keep.tile([P, 2 * CHUNK], U32, name=f"y_codes{u}", align_bytes=64) for u in range(2)]
-        step, y, y_bf = {}, {}, {}
+        y_bf = [keep.tile([P, PACK * 2 * CHUNK], BF16, name=f"y_bf{u}", align_bytes=64) for u in range(2)]
+        step = {}
 
         def mul(q):
             step[q] = keep.tile([P, PACK, CHUNK], F32, name=f"step{q}")
             nc.vector.scalar_tensor_tensor(step[q][:], gates[q][:], 1.0, diff[:, :, q * CHUNK : (q + 1) * CHUNK], ALU.add, ALU.mult)
 
+        def views(q, y):
+            u, v = divmod(q, 2)
+            dst = y_bf[u][:, v * PACK * CHUNK : (v + 1) * PACK * CHUNK].rearrange("p (c i t) -> p c t i", i=4, t=PACK)
+            return dst, y[:].rearrange("p t (c i) -> p c t i", i=4)
+
         def add(q):
             places = slice(q * CHUNK, (q + 1) * CHUNK)
-            y[q] = keep.tile([P, PACK, CHUNK], F32, name=f"y{q}")
-            nc.vector.scalar_tensor_tensor(y[q][:], step[q][:], 0.5, state_t[:, :, places], ALU.mult, ALU.add)
-            nc.sync.dma_start(out=out_rows[:, :, places], in_=y[q][:])
-            y_bf[q] = keep.tile([P, PACK * CHUNK], BF16, name=f"y_bf{q}", align_bytes=64)
-            dst = y_bf[q][:].rearrange("p (c i t) -> p c t i", i=4, t=PACK)
-            src = y[q][:].rearrange("p t (c i) -> p c t i", i=4)
-            if q < CHUNKS - 1:
-                nc.scalar.activation(dst, src, ACT.Copy)
-            else:
-                nc.vector.tensor_copy(dst, src)
+            y = keep.tile([P, PACK, CHUNK], F32, name=f"y{q}")
+            nc.vector.scalar_tensor_tensor(y[:], step[q][:], 0.5, state_t[:, :, places], ALU.mult, ALU.add)
+            nc.sync.dma_start(out=out_rows[:, :, places], in_=y[:])
+            dst, src = views(q, y)
+            share = CHUNK // 4 if q < CHUNKS - 1 else CHUNK // 8
+            nc.scalar.activation(dst[:, :share], src[:, :share], ACT.Copy)
+            return dst[:, share:], src[:, share:]
 
-        def pack(q):
-            u, v = divmod(q, 2)
-            nc.vector.quantize_mx(out=y_codes[u][:, v * CHUNK : (v + 1) * CHUNK].bitcast(FP8X4), scales=y_scale[:, q * CHUNK : (q + 1) * CHUNK], in_=y_bf[q][:])
-            if v == 1:
+        def pack(lo, hi):
+            u = lo // 2
+            words_at = slice((lo - 2 * u) * CHUNK, (hi - 2 * u) * CHUNK)
+            nc.vector.quantize_mx(out=y_codes[u][:, words_at].bitcast(FP8X4), scales=y_scale[:, lo * CHUNK : hi * CHUNK], in_=y_bf[u][:, PACK * words_at.start : PACK * words_at.stop])
+            if hi == 2 * u + 2:
                 nc.sync.dma_start(out=out_words[:, u * 2 * CHUNK : (u + 1) * 2 * CHUNK], in_=y_codes[u][:].bitcast(I32))
 
         mul(0)
-        for q in range(CHUNKS):
-            if q + 1 < CHUNKS:
-                mul(q + 1)
+        for q in range(CHUNKS - 1):
+            mul(q + 1)
             add(q)
-            if q >= 1:
-                pack(q - 1)
-        pack(CHUNKS - 1)
+        dst, src = add(CHUNKS - 1)
+        pack(0, 2)
+        nc.vector.tensor_copy(dst, src)
+        pack(2, 3)
+        pack(3, 4)
         for quad in range(4):
             eng = nc.scalar if quad % 2 else nc.sync
             eng.dma_start(out=out_2[0, 4 * quad : 4 * quad + 4, :].bitcast(I32), in_=y_scale[32 * quad : 32 * quad + 4, :].bitcast(I32))

@@ -1,6 +1,7 @@
 from contextlib import ExitStack
 
 import concourse.mybir as mybir
+from concourse.masks import make_identity
 
 K, T, S, N = 512, 2048, 512, 512
 FLOPS = 2 * 2 * K * N * S
@@ -19,9 +20,11 @@ P = 128
 PACK = 4
 HALF = N // 2
 SCALAR_ROWS = 44
+SCALAR_ROWS_LATE = 28
 LEAD = 768
 CHUNK = 128
-CHUNKS = S // CHUNK
+EIGHTH = S // 8
+PAIRS = (slice(0, 2), slice(2, 4))
 
 
 def tile_picked_phcell_none_po_kernel(tc, x_words, x_scales, w1, w2, st, offs, out_0, out_1, out_2):
@@ -30,6 +33,8 @@ def tile_picked_phcell_none_po_kernel(tc, x_words, x_scales, w1, w2, st, offs, o
         keep = ctx.enter_context(tc.tile_pool(name="keep", bufs=1))
         psum = ctx.enter_context(tc.psum_pool(name="psum", bufs=1))
 
+        identity = keep.tile([P, P], F32, name="identity")
+        make_identity(nc, identity[:])
         scale_table = keep.tile([P, T], U8, name="scale_table", tag="late", align_bytes=64)
         nc.vector.memset(scale_table[:].bitcast(I32), 0)
         word_table = keep.tile([P, T], U32, name="word_table", tag="last", align_bytes=64)
@@ -61,89 +66,106 @@ def tile_picked_phcell_none_po_kernel(tc, x_words, x_scales, w1, w2, st, offs, o
             nc.sync.dma_start(out=state[:, 2 * S * h : 2 * S * (h + 1)], in_=st_rows[:, 2 * S * h : 2 * S * (h + 1)])
         state_t = state[:].rearrange("p (t j) -> p t j", t=PACK)
 
-        def round_weight(grouped, raw):
+        def round_weight(grouped, raw, rows):
             dst = grouped[:].rearrange("p (t m j) -> p m t j", t=PACK, j=PACK)
             src = raw.rearrange("p (j m t) -> p m t j", j=PACK, t=PACK)
-            nc.scalar.activation(dst[:, :SCALAR_ROWS], src[:, :SCALAR_ROWS], ACT.Copy)
-            nc.vector.tensor_copy(dst[:, SCALAR_ROWS:], src[:, SCALAR_ROWS:])
+            nc.scalar.activation(dst[:, :rows], src[:, :rows], ACT.Copy)
+            nc.vector.tensor_copy(dst[:, rows:], src[:, rows:])
 
         w2_bf = keep.tile([P, PACK * N], BF16, name="w2_bf", align_bytes=64)
-        w1_bf = keep.tile([P, PACK * N], BF16, name="w1_bf", align_bytes=64)
-        round_weight(w2_bf, w2_raw[:])
+        w1_bf = keep.tile([P, PACK * N], BF16, name="w1_bf", tag="rounded", align_bytes=64)
+        round_weight(w2_bf, w2_raw[:], SCALAR_ROWS)
         w2_codes = keep.tile([P, N], U32, name="w2_codes", align_bytes=64)
         w2_scale = keep.tile([P, N], U8, name="w2_scale", align_bytes=64)
         for u in range(2):
             nc.vector.quantize_mx(out=w2_codes[:, u * HALF : (u + 1) * HALF].bitcast(FP8X4), scales=w2_scale[:, u * HALF : (u + 1) * HALF], in_=w2_bf[:, u * 1024 : (u + 1) * 1024])
-        round_weight(w1_bf, w1_raw[:])
-        new = keep.tile([P, PACK, S], F32, name="new", tag="late", align_bytes=64)
-        for t in range(PACK):
-            cols = slice(t * P, (t + 1) * P)
-            bank = psum.tile([P, S], F32, name=f"new_bank{t}")
-            nc.tensor.matmul_mx(out=bank[:], lhsT=w2_codes[:, cols].bitcast(FP8X4), lhsT_scale=w2_scale[:, cols], rhs=x_codes[:].bitcast(FP8X4), rhs_scale=x_scale[:], start=True, stop=True)
-            nc.scalar.activation(new[:, t, :], bank[:], ACT.Tanh)
+        round_weight(w1_bf, w1_raw[:], SCALAR_ROWS_LATE)
         w1_codes = keep.tile([P, N], U32, name="w1_codes", align_bytes=64)
         w1_scale = keep.tile([P, N], U8, name="w1_scale", align_bytes=64)
-        nc.vector.quantize_mx(out=w1_codes[:].bitcast(FP8X4), scales=w1_scale[:], in_=w1_bf[:])
+        for u in range(2):
+            nc.vector.quantize_mx(out=w1_codes[:, u * HALF : (u + 1) * HALF].bitcast(FP8X4), scales=w1_scale[:, u * HALF : (u + 1) * HALF], in_=w1_bf[:, u * 1024 : (u + 1) * 1024])
 
-        diff = keep.tile([P, PACK, S], F32, name="diff")
-        for t in range(PACK - 1):
-            nc.vector.tensor_tensor(diff[:, t, :], new[:, t, :], state_t[:, t, :], ALU.subtract)
-        for places in (slice(0, S // 2), slice(S // 2, S)):
-            nc.vector.tensor_tensor(diff[:, PACK - 1, places], new[:, PACK - 1, places], state_t[:, PACK - 1, places], ALU.subtract)
+        def product(codes, scales, h, u, bank_tag, result, scale):
+            places = slice(h * HALF, (h + 1) * HALF)
+            bank = psum.tile([P, 2, HALF], F32, name=f"{bank_tag}_{h}", tag=bank_tag)
+            for i in range(2):
+                cols = slice((2 * u + i) * P, (2 * u + i + 1) * P)
+                nc.tensor.matmul_mx(out=bank[:, i, :], lhsT=codes[:, cols].bitcast(FP8X4), lhsT_scale=scales[:, cols], rhs=x_codes[:, places].bitcast(FP8X4), rhs_scale=x_scale[:, places], start=True, stop=True)
+            nc.scalar.activation(result, bank[:], ACT.Tanh, scale=scale)
 
-        gates = []
-        for q in range(CHUNKS):
-            places = slice(q * CHUNK, (q + 1) * CHUNK)
-            bank = psum.tile([P, PACK, CHUNK], F32, name=f"gate_bank{q}")
-            for t in range(PACK):
-                cols = slice(t * P, (t + 1) * P)
-                nc.tensor.matmul_mx(out=bank[:, t, :], lhsT=w1_codes[:, cols].bitcast(FP8X4), lhsT_scale=w1_scale[:, cols], rhs=x_codes[:, places].bitcast(FP8X4), rhs_scale=x_scale[:, places], start=True, stop=True)
-            gate = keep.tile([P, PACK, CHUNK], F32, name=f"gate{q}")
-            nc.scalar.activation(gate[:], bank[:], ACT.Tanh, scale=0.5)
-            gates.append(gate)
+        rooms = [w1_raw[:, r * S : (r + 1) * S].rearrange("p (i j) -> p i j", i=2) for r in range(3)]
+        early = keep.tile([P, 2, HALF], F32, name="early")
+        minus_first = (rooms[0], rooms[1])
+        minus = (early[:], rooms[2])
+        product(w2_codes, w2_scale, 1, 0, "new_bank2", minus[0], -1.0)
+        product(w2_codes, w2_scale, 0, 0, "new_bank0", minus_first[0], -1.0)
+        product(w2_codes, w2_scale, 0, 1, "new_bank1", minus_first[1], -1.0)
+        product(w2_codes, w2_scale, 1, 1, "new_bank3", minus[1], -1.0)
+        gate = keep.tile([P, PACK, HALF], F32, name="gate")
+        for u in range(2):
+            product(w1_codes, w1_scale, 0, u, f"gate_bank{u}", gate[:, PAIRS[u], :], 0.5)
+        diff = keep.tile([P, PACK, HALF], F32, name="diff", tag="rounded", align_bytes=64)
+        for u in range(2):
+            nc.vector.tensor_tensor(diff[:, PAIRS[u], :], minus_first[u], state_t[:, PAIRS[u], :HALF], ALU.add)
+        turned_gates = []
+        for q in range(2):
+            places = slice(HALF + q * CHUNK, HALF + (q + 1) * CHUNK)
+            bank = psum.tile([P, N], F32, name=f"turned_gate_bank{q}")
+            nc.tensor.matmul_mx(out=bank[:], lhsT=x_codes[:, places].bitcast(FP8X4), lhsT_scale=x_scale[:, places], rhs=w1_codes[:].bitcast(FP8X4), rhs_scale=w1_scale[:], start=True, stop=True)
+            turned_gate = keep.tile([P, N], F32, name=f"turned_gate{q}", tag=f"y{CHUNK * q + 1 - q}")
+            nc.scalar.activation(turned_gate[:], bank[:], ACT.Tanh, scale=0.5)
+            turned_gates.append(turned_gate)
+        turned_diff = [psum.tile([P, N], F32, name=f"turned_diff{q}", tag=f"new_bank{q}") for q in range(2)]
+        for u in range(2):
+            for q in range(2):
+                for i in range(2):
+                    cols = slice((2 * u + i) * P, (2 * u + i + 1) * P)
+                    nc.tensor.matmul(turned_diff[q][:, cols], lhsT=state_t[:, 2 * u + i, HALF + q * CHUNK : HALF + (q + 1) * CHUNK], rhs=identity[:], is_transpose=True, start=True, stop=False)
+                    nc.tensor.matmul(turned_diff[q][:, cols], lhsT=minus[u][:, i, q * CHUNK : (q + 1) * CHUNK], rhs=identity[:], is_transpose=True, start=False, stop=True)
 
         out_rows = out_0.rearrange("(p t) j -> p t j", t=PACK)
         out_words = out_1[0].rearrange("p c r -> p (c r)").bitcast(I32)
         y_scale = keep.tile([P, S], U8, name="y_scale", align_bytes=64)
-        y_codes = [keep.tile([P, 2 * CHUNK], U32, name=f"y_codes{u}", align_bytes=64) for u in range(2)]
-        y_bf = [keep.tile([P, PACK * 2 * CHUNK], BF16, name=f"y_bf{u}", align_bytes=64) for u in range(2)]
-        step = {}
+        y_codes = [keep.tile([P, HALF], U32, name=f"y_codes{u}", align_bytes=64) for u in range(2)]
+        y_bf = [keep.tile([P, PACK * HALF], BF16, name=f"y_bf{u}", align_bytes=64) for u in range(2)]
 
-        def mul(q):
-            step[q] = keep.tile([P, PACK, CHUNK], F32, name=f"step{q}")
-            nc.vector.scalar_tensor_tensor(step[q][:], gates[q][:], 1.0, diff[:, :, q * CHUNK : (q + 1) * CHUNK], ALU.add, ALU.mult)
-
-        def views(q, y):
-            u, v = divmod(q, 2)
-            dst = y_bf[u][:, v * PACK * CHUNK : (v + 1) * PACK * CHUNK].rearrange("p (c i t) -> p c t i", i=4, t=PACK)
+        def finish(step, lo, hi):
+            h, at = divmod(lo, HALF)
+            y = keep.tile([P, PACK, hi - lo], F32, name=f"y{lo}", tag=f"y{lo}")
+            nc.vector.scalar_tensor_tensor(y[:], step, -0.5, state_t[:, :, lo:hi], ALU.mult, ALU.add)
+            nc.sync.dma_start(out=out_rows[:, :, lo:hi], in_=y[:])
+            dst = y_bf[h][:, PACK * at : PACK * (at + hi - lo)].rearrange("p (c i t) -> p c t i", i=4, t=PACK)
             return dst, y[:].rearrange("p t (c i) -> p c t i", i=4)
 
-        def add(q):
-            places = slice(q * CHUNK, (q + 1) * CHUNK)
-            y = keep.tile([P, PACK, CHUNK], F32, name=f"y{q}")
-            nc.vector.scalar_tensor_tensor(y[:], step[q][:], 0.5, state_t[:, :, places], ALU.mult, ALU.add)
-            nc.sync.dma_start(out=out_rows[:, :, places], in_=y[:])
-            dst, src = views(q, y)
-            share = CHUNK // 4 if q < CHUNKS - 1 else CHUNK // 8
-            nc.scalar.activation(dst[:, :share], src[:, :share], ACT.Copy)
-            return dst[:, share:], src[:, share:]
-
         def pack(lo, hi):
-            u = lo // 2
-            words_at = slice((lo - 2 * u) * CHUNK, (hi - 2 * u) * CHUNK)
-            nc.vector.quantize_mx(out=y_codes[u][:, words_at].bitcast(FP8X4), scales=y_scale[:, lo * CHUNK : hi * CHUNK], in_=y_bf[u][:, PACK * words_at.start : PACK * words_at.stop])
-            if hi == 2 * u + 2:
-                nc.sync.dma_start(out=out_words[:, u * 2 * CHUNK : (u + 1) * 2 * CHUNK], in_=y_codes[u][:].bitcast(I32))
+            h, at = divmod(lo, HALF)
+            nc.vector.quantize_mx(out=y_codes[h][:, at : at + hi - lo].bitcast(FP8X4), scales=y_scale[:, lo:hi], in_=y_bf[h][:, PACK * at : PACK * (at + hi - lo)])
 
-        mul(0)
-        for q in range(CHUNKS - 1):
-            mul(q + 1)
-            add(q)
-        dst, src = add(CHUNKS - 1)
-        pack(0, 2)
-        nc.vector.tensor_copy(dst, src)
-        pack(2, 3)
-        pack(3, 4)
+        step = keep.tile([P, PACK, HALF], F32, name="step")
+        for pair in PAIRS:
+            nc.vector.scalar_tensor_tensor(step[:, pair, :], gate[:, pair, :], 1.0, diff[:, pair, :], ALU.add, ALU.mult)
+        dst, src = finish(step[:, :, :CHUNK], 0, CHUNK)
+        nc.scalar.activation(dst, src, ACT.Copy)
+        backs = []
+        for q in range(2):
+            turned_step = keep.tile([P, N], F32, name=f"turned_step{q}")
+            nc.vector.scalar_tensor_tensor(turned_step[:], turned_gates[q][:], 1.0, turned_diff[q][:], ALU.add, ALU.mult)
+            back = psum.tile([P, PACK, CHUNK], F32, name=f"back{q}", tag=f"gate_bank{q}")
+            for t in range(PACK):
+                nc.tensor.transpose(back[:, t, :], turned_step[:, t * P : (t + 1) * P], identity[:])
+            backs.append(back)
+        dst, src = finish(step[:, :, CHUNK:], CHUNK, HALF)
+        nc.scalar.activation(dst, src, ACT.Copy)
+        dst, src = finish(backs[0][:], HALF, HALF + CHUNK)
+        nc.scalar.activation(dst, src, ACT.Copy)
+        dst, src = finish(backs[1][:], HALF + CHUNK, S)
+        nc.scalar.activation(dst[:, : CHUNK // 8], src[:, : CHUNK // 8], ACT.Copy)
+        pack(0, HALF)
+        nc.sync.dma_start(out=out_words[:, :HALF], in_=y_codes[0][:].bitcast(I32))
+        nc.vector.tensor_copy(dst[:, CHUNK // 8 :], src[:, CHUNK // 8 :])
+        pack(HALF, HALF + CHUNK)
+        pack(HALF + CHUNK, S)
+        nc.sync.dma_start(out=out_words[:, HALF:], in_=y_codes[1][:].bitcast(I32))
         for quad in range(4):
             eng = nc.scalar if quad % 2 else nc.sync
             eng.dma_start(out=out_2[0, 4 * quad : 4 * quad + 4, :].bitcast(I32), in_=y_scale[32 * quad : 32 * quad + 4, :].bitcast(I32))

@@ -20,7 +20,7 @@ P = 128
 PACK = 4
 HALF = N // 2
 SCALAR_ROWS = 44
-SCALAR_ROWS_LATE = 28
+SCALAR_ROWS_LATE = 38
 LEAD = 768
 CHUNK = 128
 EIGHTH = S // 8
@@ -33,52 +33,55 @@ def tile_picked_phcell_none_po_kernel(tc, x_words, x_scales, w1, w2, st, offs, o
         keep = ctx.enter_context(tc.tile_pool(name="keep", bufs=1))
         psum = ctx.enter_context(tc.psum_pool(name="psum", bufs=1))
 
-        identity = keep.tile([P, P], F32, name="identity")
-        make_identity(nc, identity[:])
         scale_table = keep.tile([P, T], U8, name="scale_table", tag="late", align_bytes=64)
         nc.vector.memset(scale_table[:].bitcast(I32), 0)
-        word_table = keep.tile([P, T], U32, name="word_table", tag="last", align_bytes=64)
-        words = x_words[0].rearrange("p c r -> p (c r)").bitcast(I32)
+        w2_raw = keep.tile([P, PACK * N], F32, name="w2_raw", tag="last", align_bytes=64)
+        w2_rows = w2.rearrange("(p j) c -> p (j c)", j=PACK)
         for cols in (slice(0, 512), slice(512, LEAD)):
-            nc.sync.dma_start(out=word_table[:, cols].bitcast(I32), in_=words[:, cols])
+            nc.sync.dma_start(out=w2_raw[:, cols], in_=w2_rows[:, cols])
         offsets = keep.tile([P, S // 16], U16, name="offsets")
         nc.sync.dma_start(offsets[:], offs)
         nc.sync.dma_start(out=scale_table[0:P:8, :].bitcast(I32), in_=x_scales[0].bitcast(I32))
-        nc.sync.dma_start(out=word_table[:, LEAD:].bitcast(I32), in_=words[:, LEAD:])
+        nc.sync.dma_start(out=w2_raw[:, LEAD:], in_=w2_rows[:, LEAD:])
+        word_table = keep.tile([P, T], U32, name="word_table", tag="rounded", align_bytes=64)
+        nc.sync.dma_start(out=word_table[:].bitcast(I32), in_=x_words[0].rearrange("p c r -> p (c r)").bitcast(I32))
         x_scale = keep.tile([P, S], U8, name="x_scale", align_bytes=64)
         nc.vector.memset(x_scale[:].bitcast(I32), 0)
-
-        w2_raw = keep.tile([P, PACK * N], F32, name="w2_raw")
-        nc.sync.dma_start(out=w2_raw[:], in_=w2.rearrange("(p j) c -> p (j c)", j=PACK))
+        identity = keep.tile([P, P], F32, name="identity")
+        nc.vector.memset(identity[:], 0.0)
+        warm = keep.tile([P, 1], F32, name="warm")
+        nc.scalar.activation(warm[:], identity[:, 0:1], ACT.Tanh)
+        make_identity(nc, identity[:], nomemset=True)
 
         picked_scales = keep.tile([P, S], U8, name="picked_scales", align_bytes=64)
         nc.vector.tensor_copy(picked_scales[:], scale_table[:].indirect(offsets[:]))
         for i in range(4):
             nc.sync.dma_start(out=x_scale[i:P:32, :].bitcast(I32), in_=picked_scales[8 * i : P : 32, :].bitcast(I32))
-        x_codes = keep.tile([P, S], U32, name="x_codes", align_bytes=64)
-        nc.vector.tensor_copy(x_codes[:], word_table[:].indirect(offsets[:]))
 
         w1_raw = keep.tile([P, PACK * N], F32, name="w1_raw", tag="late", align_bytes=64)
         nc.sync.dma_start(out=w1_raw[:], in_=w1.rearrange("(p j) c -> p (j c)", j=PACK))
-        state = keep.tile([P, PACK * S], F32, name="state", tag="last", align_bytes=64)
-        st_rows = st.rearrange("(p t) j -> p (t j)", t=PACK)
-        for h in range(2):
-            nc.sync.dma_start(out=state[:, 2 * S * h : 2 * S * (h + 1)], in_=st_rows[:, 2 * S * h : 2 * S * (h + 1)])
-        state_t = state[:].rearrange("p (t j) -> p t j", t=PACK)
-
         def round_weight(grouped, raw, rows):
             dst = grouped[:].rearrange("p (t m j) -> p m t j", t=PACK, j=PACK)
             src = raw.rearrange("p (j m t) -> p m t j", j=PACK, t=PACK)
             nc.scalar.activation(dst[:, :rows], src[:, :rows], ACT.Copy)
             nc.vector.tensor_copy(dst[:, rows:], src[:, rows:])
 
-        w2_bf = keep.tile([P, PACK * N], BF16, name="w2_bf", align_bytes=64)
-        w1_bf = keep.tile([P, PACK * N], BF16, name="w1_bf", tag="rounded", align_bytes=64)
+        w2_bf = keep.tile([P, PACK * N], BF16, name="w2_bf", tag="picked", align_bytes=64)
         round_weight(w2_bf, w2_raw[:], SCALAR_ROWS)
+        state = keep.tile([P, PACK * S], F32, name="state", tag="last", align_bytes=64)
+        st_rows = st.rearrange("(p t) j -> p (t j)", t=PACK)
+        for h in range(2):
+            nc.sync.dma_start(out=state[:, 2 * S * h : 2 * S * (h + 1)], in_=st_rows[:, 2 * S * h : 2 * S * (h + 1)])
+        state_t = state[:].rearrange("p (t j) -> p t j", t=PACK)
+
         w2_codes = keep.tile([P, N], U32, name="w2_codes", align_bytes=64)
         w2_scale = keep.tile([P, N], U8, name="w2_scale", align_bytes=64)
         for u in range(2):
             nc.vector.quantize_mx(out=w2_codes[:, u * HALF : (u + 1) * HALF].bitcast(FP8X4), scales=w2_scale[:, u * HALF : (u + 1) * HALF], in_=w2_bf[:, u * 1024 : (u + 1) * 1024])
+        x_codes = keep.tile([P, S], U32, name="x_codes", tag="picked", align_bytes=64)
+        for h in (1, 0):
+            nc.vector.tensor_copy(x_codes[:, h * HALF : (h + 1) * HALF], word_table[:].indirect(offsets[:, h * HALF // 16 : (h + 1) * HALF // 16]))
+        w1_bf = keep.tile([P, PACK * N], BF16, name="w1_bf", tag="rounded", align_bytes=64)
         round_weight(w1_bf, w1_raw[:], SCALAR_ROWS_LATE)
         w1_codes = keep.tile([P, N], U32, name="w1_codes", align_bytes=64)
         w1_scale = keep.tile([P, N], U8, name="w1_scale", align_bytes=64)
@@ -93,14 +96,13 @@ def tile_picked_phcell_none_po_kernel(tc, x_words, x_scales, w1, w2, st, offs, o
                 nc.tensor.matmul_mx(out=bank[:, i, :], lhsT=codes[:, cols].bitcast(FP8X4), lhsT_scale=scales[:, cols], rhs=x_codes[:, places].bitcast(FP8X4), rhs_scale=x_scale[:, places], start=True, stop=True)
             nc.scalar.activation(result, bank[:], ACT.Tanh, scale=scale)
 
-        rooms = [w1_raw[:, r * S : (r + 1) * S].rearrange("p (i j) -> p i j", i=2) for r in range(3)]
-        early = keep.tile([P, 2, HALF], F32, name="early")
-        minus_first = (rooms[0], rooms[1])
-        minus = (early[:], rooms[2])
-        product(w2_codes, w2_scale, 1, 0, "new_bank2", minus[0], -1.0)
-        product(w2_codes, w2_scale, 0, 0, "new_bank0", minus_first[0], -1.0)
-        product(w2_codes, w2_scale, 0, 1, "new_bank1", minus_first[1], -1.0)
-        product(w2_codes, w2_scale, 1, 1, "new_bank3", minus[1], -1.0)
+        minus_first = [w1_raw[:, r * S : (r + 1) * S].rearrange("p (i j) -> p i j", i=2) for r in range(2)]
+        early = keep.tile([P, PACK, HALF], F32, name="early")
+        minus = [early[:, pair, :] for pair in PAIRS]
+        for u in range(2):
+            product(w2_codes, w2_scale, 1, u, f"new_bank{2 + u}", minus[u], -1.0)
+        for u in range(2):
+            product(w2_codes, w2_scale, 0, u, f"new_bank{u}", minus_first[u], -1.0)
         gate = keep.tile([P, PACK, HALF], F32, name="gate")
         for u in range(2):
             product(w1_codes, w1_scale, 0, u, f"gate_bank{u}", gate[:, PAIRS[u], :], 0.5)
@@ -112,12 +114,12 @@ def tile_picked_phcell_none_po_kernel(tc, x_words, x_scales, w1, w2, st, offs, o
             places = slice(HALF + q * CHUNK, HALF + (q + 1) * CHUNK)
             bank = psum.tile([P, N], F32, name=f"turned_gate_bank{q}")
             nc.tensor.matmul_mx(out=bank[:], lhsT=x_codes[:, places].bitcast(FP8X4), lhsT_scale=x_scale[:, places], rhs=w1_codes[:].bitcast(FP8X4), rhs_scale=w1_scale[:], start=True, stop=True)
-            turned_gate = keep.tile([P, N], F32, name=f"turned_gate{q}", tag=f"y{CHUNK * q + 1 - q}")
+            turned_gate = keep.tile([P, N], F32, name=f"turned_gate{q}", tag=f"y{CHUNK * q}")
             nc.scalar.activation(turned_gate[:], bank[:], ACT.Tanh, scale=0.5)
             turned_gates.append(turned_gate)
         turned_diff = [psum.tile([P, N], F32, name=f"turned_diff{q}", tag=f"new_bank{q}") for q in range(2)]
-        for u in range(2):
-            for q in range(2):
+        for q in range(2):
+            for u in range(2):
                 for i in range(2):
                     cols = slice((2 * u + i) * P, (2 * u + i + 1) * P)
                     nc.tensor.matmul(turned_diff[q][:, cols], lhsT=state_t[:, 2 * u + i, HALF + q * CHUNK : HALF + (q + 1) * CHUNK], rhs=identity[:], is_transpose=True, start=True, stop=False)
@@ -144,8 +146,6 @@ def tile_picked_phcell_none_po_kernel(tc, x_words, x_scales, w1, w2, st, offs, o
         step = keep.tile([P, PACK, HALF], F32, name="step")
         for pair in PAIRS:
             nc.vector.scalar_tensor_tensor(step[:, pair, :], gate[:, pair, :], 1.0, diff[:, pair, :], ALU.add, ALU.mult)
-        dst, src = finish(step[:, :, :CHUNK], 0, CHUNK)
-        nc.scalar.activation(dst, src, ACT.Copy)
         backs = []
         for q in range(2):
             turned_step = keep.tile([P, N], F32, name=f"turned_step{q}")
@@ -154,8 +154,9 @@ def tile_picked_phcell_none_po_kernel(tc, x_words, x_scales, w1, w2, st, offs, o
             for t in range(PACK):
                 nc.tensor.transpose(back[:, t, :], turned_step[:, t * P : (t + 1) * P], identity[:])
             backs.append(back)
-        dst, src = finish(step[:, :, CHUNK:], CHUNK, HALF)
-        nc.scalar.activation(dst, src, ACT.Copy)
+        for q in range(2):
+            dst, src = finish(step[:, :, q * CHUNK : (q + 1) * CHUNK], q * CHUNK, (q + 1) * CHUNK)
+            nc.scalar.activation(dst, src, ACT.Copy)
         dst, src = finish(backs[0][:], HALF, HALF + CHUNK)
         nc.scalar.activation(dst, src, ACT.Copy)
         dst, src = finish(backs[1][:], HALF + CHUNK, S)

@@ -20,7 +20,6 @@ P = 128
 PACK = 4
 HALF = N // 2
 SCALAR_ROWS = 44
-SCALAR_ROWS_LATE = 38
 LEAD = 768
 CHUNK = 128
 EIGHTH = S // 8
@@ -79,14 +78,13 @@ def tile_picked_phcell_none_po_kernel(tc, x_words, x_scales, w1, w2, st, offs, o
         for u in range(2):
             nc.vector.quantize_mx(out=w2_codes[:, u * HALF : (u + 1) * HALF].bitcast(FP8X4), scales=w2_scale[:, u * HALF : (u + 1) * HALF], in_=w2_bf[:, u * 1024 : (u + 1) * 1024])
         x_codes = keep.tile([P, S], U32, name="x_codes", tag="picked", align_bytes=64)
-        for h in (1, 0):
+        for h in range(2):
             nc.vector.tensor_copy(x_codes[:, h * HALF : (h + 1) * HALF], word_table[:].indirect(offsets[:, h * HALF // 16 : (h + 1) * HALF // 16]))
         w1_bf = keep.tile([P, PACK * N], BF16, name="w1_bf", tag="rounded", align_bytes=64)
-        round_weight(w1_bf, w1_raw[:], SCALAR_ROWS_LATE)
+        round_weight(w1_bf, w1_raw[:], SCALAR_ROWS)
         w1_codes = keep.tile([P, N], U32, name="w1_codes", align_bytes=64)
         w1_scale = keep.tile([P, N], U8, name="w1_scale", align_bytes=64)
-        for u in range(2):
-            nc.vector.quantize_mx(out=w1_codes[:, u * HALF : (u + 1) * HALF].bitcast(FP8X4), scales=w1_scale[:, u * HALF : (u + 1) * HALF], in_=w1_bf[:, u * 1024 : (u + 1) * 1024])
+        nc.vector.quantize_mx(out=w1_codes[:].bitcast(FP8X4), scales=w1_scale[:], in_=w1_bf[:])
 
         def product(codes, scales, h, u, bank_tag, result, scale):
             places = slice(h * HALF, (h + 1) * HALF)
@@ -96,34 +94,38 @@ def tile_picked_phcell_none_po_kernel(tc, x_words, x_scales, w1, w2, st, offs, o
                 nc.tensor.matmul_mx(out=bank[:, i, :], lhsT=codes[:, cols].bitcast(FP8X4), lhsT_scale=scales[:, cols], rhs=x_codes[:, places].bitcast(FP8X4), rhs_scale=x_scale[:, places], start=True, stop=True)
             nc.scalar.activation(result, bank[:], ACT.Tanh, scale=scale)
 
-        minus_first = [w1_raw[:, r * S : (r + 1) * S].rearrange("p (i j) -> p i j", i=2) for r in range(2)]
-        early = keep.tile([P, PACK, HALF], F32, name="early")
-        minus = [early[:, pair, :] for pair in PAIRS]
-        for u in range(2):
-            product(w2_codes, w2_scale, 1, u, f"new_bank{2 + u}", minus[u], -1.0)
+        early = keep.tile([P, 2, HALF], F32, name="early")
+        minus_first = (early[:], w1_raw[:, :S].rearrange("p (i j) -> p i j", i=2))
+        minus_second = w1_raw[:, S : 3 * S].rearrange("p (t j) -> p t j", t=PACK)
         for u in range(2):
             product(w2_codes, w2_scale, 0, u, f"new_bank{u}", minus_first[u], -1.0)
+        for u in range(2):
+            product(w2_codes, w2_scale, 1, u, f"new_bank{2 + u}", minus_second[:, PAIRS[u], :], -1.0)
         gate = keep.tile([P, PACK, HALF], F32, name="gate")
         for u in range(2):
             product(w1_codes, w1_scale, 0, u, f"gate_bank{u}", gate[:, PAIRS[u], :], 0.5)
         diff = keep.tile([P, PACK, HALF], F32, name="diff", tag="rounded", align_bytes=64)
         for u in range(2):
             nc.vector.tensor_tensor(diff[:, PAIRS[u], :], minus_first[u], state_t[:, PAIRS[u], :HALF], ALU.add)
-        turned_gates = []
-        for q in range(2):
-            places = slice(HALF + q * CHUNK, HALF + (q + 1) * CHUNK)
-            bank = psum.tile([P, N], F32, name=f"turned_gate_bank{q}")
-            nc.tensor.matmul_mx(out=bank[:], lhsT=x_codes[:, places].bitcast(FP8X4), lhsT_scale=x_scale[:, places], rhs=w1_codes[:].bitcast(FP8X4), rhs_scale=w1_scale[:], start=True, stop=True)
-            turned_gate = keep.tile([P, N], F32, name=f"turned_gate{q}", tag=f"y{CHUNK * q}")
-            nc.scalar.activation(turned_gate[:], bank[:], ACT.Tanh, scale=0.5)
-            turned_gates.append(turned_gate)
-        turned_diff = [psum.tile([P, N], F32, name=f"turned_diff{q}", tag=f"new_bank{q}") for q in range(2)]
-        for q in range(2):
-            for u in range(2):
-                for i in range(2):
-                    cols = slice((2 * u + i) * P, (2 * u + i + 1) * P)
-                    nc.tensor.matmul(turned_diff[q][:, cols], lhsT=state_t[:, 2 * u + i, HALF + q * CHUNK : HALF + (q + 1) * CHUNK], rhs=identity[:], is_transpose=True, start=True, stop=False)
-                    nc.tensor.matmul(turned_diff[q][:, cols], lhsT=minus[u][:, i, q * CHUNK : (q + 1) * CHUNK], rhs=identity[:], is_transpose=True, start=False, stop=True)
+        third = slice(HALF, HALF + CHUNK)
+        last = slice(HALF + CHUNK, S)
+        diff_third = keep.tile([P, PACK, CHUNK], F32, name="diff_third")
+        nc.vector.tensor_tensor(diff_third[:], minus_second[:, :, :CHUNK], state_t[:, :, third], ALU.add)
+        bank = psum.tile([P, PACK, CHUNK], F32, name="third_gate_bank")
+        for t in range(PACK):
+            cols = slice(t * P, (t + 1) * P)
+            nc.tensor.matmul_mx(out=bank[:, t, :], lhsT=w1_codes[:, cols].bitcast(FP8X4), lhsT_scale=w1_scale[:, cols], rhs=x_codes[:, third].bitcast(FP8X4), rhs_scale=x_scale[:, third], start=True, stop=True)
+        gate_third = keep.tile([P, PACK, CHUNK], F32, name="gate_third")
+        nc.scalar.activation(gate_third[:], bank[:], ACT.Tanh, scale=0.5)
+        bank = psum.tile([P, N], F32, name="turned_gate_bank")
+        nc.tensor.matmul_mx(out=bank[:], lhsT=x_codes[:, last].bitcast(FP8X4), lhsT_scale=x_scale[:, last], rhs=w1_codes[:].bitcast(FP8X4), rhs_scale=w1_scale[:], start=True, stop=True)
+        turned_gate = keep.tile([P, N], F32, name="turned_gate", tag=f"y{CHUNK}")
+        nc.scalar.activation(turned_gate[:], bank[:], ACT.Tanh, scale=0.5)
+        turned_diff = psum.tile([P, N], F32, name="turned_diff", tag="new_bank1")
+        for t in range(PACK):
+            cols = slice(t * P, (t + 1) * P)
+            nc.tensor.matmul(turned_diff[:, cols], lhsT=state_t[:, t, last], rhs=identity[:], is_transpose=True, start=True, stop=False)
+            nc.tensor.matmul(turned_diff[:, cols], lhsT=minus_second[:, t, CHUNK:], rhs=identity[:], is_transpose=True, start=False, stop=True)
 
         out_rows = out_0.rearrange("(p t) j -> p t j", t=PACK)
         out_words = out_1[0].rearrange("p c r -> p (c r)").bitcast(I32)
@@ -146,20 +148,20 @@ def tile_picked_phcell_none_po_kernel(tc, x_words, x_scales, w1, w2, st, offs, o
         step = keep.tile([P, PACK, HALF], F32, name="step")
         for pair in PAIRS:
             nc.vector.scalar_tensor_tensor(step[:, pair, :], gate[:, pair, :], 1.0, diff[:, pair, :], ALU.add, ALU.mult)
-        backs = []
-        for q in range(2):
-            turned_step = keep.tile([P, N], F32, name=f"turned_step{q}")
-            nc.vector.scalar_tensor_tensor(turned_step[:], turned_gates[q][:], 1.0, turned_diff[q][:], ALU.add, ALU.mult)
-            back = psum.tile([P, PACK, CHUNK], F32, name=f"back{q}", tag=f"gate_bank{q}")
-            for t in range(PACK):
-                nc.tensor.transpose(back[:, t, :], turned_step[:, t * P : (t + 1) * P], identity[:])
-            backs.append(back)
-        for q in range(2):
-            dst, src = finish(step[:, :, q * CHUNK : (q + 1) * CHUNK], q * CHUNK, (q + 1) * CHUNK)
-            nc.scalar.activation(dst, src, ACT.Copy)
-        dst, src = finish(backs[0][:], HALF, HALF + CHUNK)
+        step_third = keep.tile([P, PACK, CHUNK], F32, name="step_third")
+        nc.vector.scalar_tensor_tensor(step_third[:], gate_third[:], 1.0, diff_third[:], ALU.add, ALU.mult)
+        dst, src = finish(step[:, :, :CHUNK], 0, CHUNK)
         nc.scalar.activation(dst, src, ACT.Copy)
-        dst, src = finish(backs[1][:], HALF + CHUNK, S)
+        turned_step = keep.tile([P, N], F32, name="turned_step")
+        nc.vector.scalar_tensor_tensor(turned_step[:], turned_gate[:], 1.0, turned_diff[:], ALU.add, ALU.mult)
+        back = psum.tile([P, PACK, CHUNK], F32, name="back", tag="new_bank3")
+        for t in range(PACK):
+            nc.tensor.transpose(back[:, t, :], turned_step[:, t * P : (t + 1) * P], identity[:])
+        dst, src = finish(step[:, :, CHUNK:], CHUNK, HALF)
+        nc.scalar.activation(dst, src, ACT.Copy)
+        dst, src = finish(step_third[:], third.start, third.stop)
+        nc.scalar.activation(dst, src, ACT.Copy)
+        dst, src = finish(back[:], last.start, last.stop)
         nc.scalar.activation(dst[:, : CHUNK // 8], src[:, : CHUNK // 8], ACT.Copy)
         pack(0, HALF)
         nc.sync.dma_start(out=out_words[:, :HALF], in_=y_codes[0][:].bitcast(I32))

@@ -22,7 +22,7 @@ HALF = N // 2
 SCALAR_ROWS = 44
 LEAD = 768
 CHUNK = 128
-EIGHTH = S // 8
+LAST_SHARE = 8
 PAIRS = (slice(0, 2), slice(2, 4))
 
 
@@ -94,6 +94,7 @@ def tile_picked_phcell_none_po_kernel(tc, x_words, x_scales, w1, w2, st, offs, o
                 nc.tensor.matmul_mx(out=bank[:, i, :], lhsT=codes[:, cols].bitcast(FP8X4), lhsT_scale=scales[:, cols], rhs=x_codes[:, places].bitcast(FP8X4), rhs_scale=x_scale[:, places], start=True, stop=True)
             nc.scalar.activation(result, bank[:], ACT.Tanh, scale=scale)
 
+        chunks = [slice(q * CHUNK, (q + 1) * CHUNK) for q in range(4)]
         early = keep.tile([P, 2, HALF], F32, name="early")
         minus_first = (early[:], w1_raw[:, :S].rearrange("p (i j) -> p i j", i=2))
         minus_second = w1_raw[:, S : 3 * S].rearrange("p (t j) -> p t j", t=PACK)
@@ -101,31 +102,34 @@ def tile_picked_phcell_none_po_kernel(tc, x_words, x_scales, w1, w2, st, offs, o
             product(w2_codes, w2_scale, 0, u, f"new_bank{u}", minus_first[u], -1.0)
         for u in range(2):
             product(w2_codes, w2_scale, 1, u, f"new_bank{2 + u}", minus_second[:, PAIRS[u], :], -1.0)
-        gate = keep.tile([P, PACK, HALF], F32, name="gate")
+        diffs = keep.tile([P, 3 * PACK * CHUNK], F32, name="diffs", tag="rounded", align_bytes=64)
+        diff_first = diffs[:, : PACK * HALF].rearrange("p (t j) -> p t j", t=PACK)
+        diff_third = diffs[:, PACK * HALF :].rearrange("p (t j) -> p t j", t=PACK)
         for u in range(2):
-            product(w1_codes, w1_scale, 0, u, f"gate_bank{u}", gate[:, PAIRS[u], :], 0.5)
-        diff = keep.tile([P, PACK, HALF], F32, name="diff", tag="rounded", align_bytes=64)
-        for u in range(2):
-            nc.vector.tensor_tensor(diff[:, PAIRS[u], :], minus_first[u], state_t[:, PAIRS[u], :HALF], ALU.add)
-        third = slice(HALF, HALF + CHUNK)
-        last = slice(HALF + CHUNK, S)
-        diff_third = keep.tile([P, PACK, CHUNK], F32, name="diff_third")
-        nc.vector.tensor_tensor(diff_third[:], minus_second[:, :, :CHUNK], state_t[:, :, third], ALU.add)
-        bank = psum.tile([P, PACK, CHUNK], F32, name="third_gate_bank")
-        for t in range(PACK):
-            cols = slice(t * P, (t + 1) * P)
-            nc.tensor.matmul_mx(out=bank[:, t, :], lhsT=w1_codes[:, cols].bitcast(FP8X4), lhsT_scale=w1_scale[:, cols], rhs=x_codes[:, third].bitcast(FP8X4), rhs_scale=x_scale[:, third], start=True, stop=True)
-        gate_third = keep.tile([P, PACK, CHUNK], F32, name="gate_third")
-        nc.scalar.activation(gate_third[:], bank[:], ACT.Tanh, scale=0.5)
+            nc.vector.tensor_tensor(diff_first[:, PAIRS[u], :], minus_first[u], state_t[:, PAIRS[u], :HALF], ALU.add)
+        nc.vector.tensor_tensor(diff_third, minus_second[:, :, :CHUNK], state_t[:, :, chunks[2]], ALU.add)
+        diff = (diff_first[:, :, chunks[0]], diff_first[:, :, chunks[1]], diff_third)
+
+        def gate_product(q):
+            bank = psum.tile([P, PACK, CHUNK], F32, name=f"gate_bank{q}")
+            for t in range(PACK):
+                cols = slice(t * P, (t + 1) * P)
+                nc.tensor.matmul_mx(out=bank[:, t, :], lhsT=w1_codes[:, cols].bitcast(FP8X4), lhsT_scale=w1_scale[:, cols], rhs=x_codes[:, chunks[q]].bitcast(FP8X4), rhs_scale=x_scale[:, chunks[q]], start=True, stop=True)
+            gate = keep.tile([P, PACK, CHUNK], F32, name=f"gate{q}")
+            nc.scalar.activation(gate[:], bank[:], ACT.Tanh, scale=0.5)
+            return gate
+
+        gates = [gate_product(q) for q in range(2)]
         bank = psum.tile([P, N], F32, name="turned_gate_bank")
-        nc.tensor.matmul_mx(out=bank[:], lhsT=x_codes[:, last].bitcast(FP8X4), lhsT_scale=x_scale[:, last], rhs=w1_codes[:].bitcast(FP8X4), rhs_scale=w1_scale[:], start=True, stop=True)
-        turned_gate = keep.tile([P, N], F32, name="turned_gate", tag=f"y{CHUNK}")
+        nc.tensor.matmul_mx(out=bank[:], lhsT=x_codes[:, chunks[3]].bitcast(FP8X4), lhsT_scale=x_scale[:, chunks[3]], rhs=w1_codes[:].bitcast(FP8X4), rhs_scale=w1_scale[:], start=True, stop=True)
+        turned_gate = keep.tile([P, N], F32, name="turned_gate")
         nc.scalar.activation(turned_gate[:], bank[:], ACT.Tanh, scale=0.5)
         turned_diff = psum.tile([P, N], F32, name="turned_diff", tag="new_bank1")
         for t in range(PACK):
             cols = slice(t * P, (t + 1) * P)
-            nc.tensor.matmul(turned_diff[:, cols], lhsT=state_t[:, t, last], rhs=identity[:], is_transpose=True, start=True, stop=False)
+            nc.tensor.matmul(turned_diff[:, cols], lhsT=state_t[:, t, chunks[3]], rhs=identity[:], is_transpose=True, start=True, stop=False)
             nc.tensor.matmul(turned_diff[:, cols], lhsT=minus_second[:, t, CHUNK:], rhs=identity[:], is_transpose=True, start=False, stop=True)
+        gates.append(gate_product(2))
 
         out_rows = out_0.rearrange("(p t) j -> p t j", t=PACK)
         out_words = out_1[0].rearrange("p c r -> p (c r)").bitcast(I32)
@@ -135,7 +139,7 @@ def tile_picked_phcell_none_po_kernel(tc, x_words, x_scales, w1, w2, st, offs, o
 
         def finish(step, lo, hi):
             h, at = divmod(lo, HALF)
-            y = keep.tile([P, PACK, hi - lo], F32, name=f"y{lo}", tag=f"y{lo}")
+            y = keep.tile([P, PACK, hi - lo], F32, name=f"y{lo}")
             nc.vector.scalar_tensor_tensor(y[:], step, -0.5, state_t[:, :, lo:hi], ALU.mult, ALU.add)
             nc.sync.dma_start(out=out_rows[:, :, lo:hi], in_=y[:])
             dst = y_bf[h][:, PACK * at : PACK * (at + hi - lo)].rearrange("p (c i t) -> p c t i", i=4, t=PACK)
@@ -145,29 +149,32 @@ def tile_picked_phcell_none_po_kernel(tc, x_words, x_scales, w1, w2, st, offs, o
             h, at = divmod(lo, HALF)
             nc.vector.quantize_mx(out=y_codes[h][:, at : at + hi - lo].bitcast(FP8X4), scales=y_scale[:, lo:hi], in_=y_bf[h][:, PACK * at : PACK * (at + hi - lo)])
 
-        step = keep.tile([P, PACK, HALF], F32, name="step")
-        for pair in PAIRS:
-            nc.vector.scalar_tensor_tensor(step[:, pair, :], gate[:, pair, :], 1.0, diff[:, pair, :], ALU.add, ALU.mult)
-        step_third = keep.tile([P, PACK, CHUNK], F32, name="step_third")
-        nc.vector.scalar_tensor_tensor(step_third[:], gate_third[:], 1.0, diff_third[:], ALU.add, ALU.mult)
-        dst, src = finish(step[:, :, :CHUNK], 0, CHUNK)
-        nc.scalar.activation(dst, src, ACT.Copy)
+        def mul(q):
+            step = keep.tile([P, PACK, CHUNK], F32, name=f"step{q}")
+            nc.vector.scalar_tensor_tensor(step[:], gates[q][:], 1.0, diff[q], ALU.add, ALU.mult)
+            return step
+
+        def finish_and_round(step, q):
+            dst, src = finish(step, chunks[q].start, chunks[q].stop)
+            nc.scalar.activation(dst, src, ACT.Copy)
+
+        steps = [mul(0), mul(1)]
+        finish_and_round(steps[0][:], 0)
         turned_step = keep.tile([P, N], F32, name="turned_step")
         nc.vector.scalar_tensor_tensor(turned_step[:], turned_gate[:], 1.0, turned_diff[:], ALU.add, ALU.mult)
         back = psum.tile([P, PACK, CHUNK], F32, name="back", tag="new_bank3")
         for t in range(PACK):
             nc.tensor.transpose(back[:, t, :], turned_step[:, t * P : (t + 1) * P], identity[:])
-        dst, src = finish(step[:, :, CHUNK:], CHUNK, HALF)
-        nc.scalar.activation(dst, src, ACT.Copy)
-        dst, src = finish(step_third[:], third.start, third.stop)
-        nc.scalar.activation(dst, src, ACT.Copy)
-        dst, src = finish(back[:], last.start, last.stop)
-        nc.scalar.activation(dst[:, : CHUNK // 8], src[:, : CHUNK // 8], ACT.Copy)
+        finish_and_round(steps[1][:], 1)
+        steps.append(mul(2))
+        finish_and_round(back[:], 3)
+        dst, src = finish(steps[2][:], chunks[2].start, chunks[2].stop)
+        nc.scalar.activation(dst[:, :LAST_SHARE], src[:, :LAST_SHARE], ACT.Copy)
         pack(0, HALF)
         nc.sync.dma_start(out=out_words[:, :HALF], in_=y_codes[0][:].bitcast(I32))
-        nc.vector.tensor_copy(dst[:, CHUNK // 8 :], src[:, CHUNK // 8 :])
-        pack(HALF, HALF + CHUNK)
-        pack(HALF + CHUNK, S)
+        nc.vector.tensor_copy(dst[:, LAST_SHARE:], src[:, LAST_SHARE:])
+        pack(chunks[3].start, chunks[3].stop)
+        pack(chunks[2].start, chunks[2].stop)
         nc.sync.dma_start(out=out_words[:, HALF:], in_=y_codes[1][:].bitcast(I32))
         for quad in range(4):
             eng = nc.scalar if quad % 2 else nc.sync

@@ -18,12 +18,12 @@ ALU = mybir.AluOpType
 
 P = 128
 PACK = 4
-HALF = N // 2
-SCALAR_ROWS = 44
-LEAD = 768
+HALF = S // 2
 CHUNK = 128
-LAST_SHARE = 8
 PAIRS = (slice(0, 2), slice(2, 4))
+LEAD = (slice(0, 512), slice(512, 768))
+SCALAR_GROUPS = 44
+SCALAR_LAST_GROUPS = 8
 
 
 def tile_picked_phcell_none_po_kernel(tc, x_words, x_scales, w1, w2, st, offs, out_0, out_1, out_2):
@@ -32,24 +32,23 @@ def tile_picked_phcell_none_po_kernel(tc, x_words, x_scales, w1, w2, st, offs, o
         keep = ctx.enter_context(tc.tile_pool(name="keep", bufs=1))
         psum = ctx.enter_context(tc.psum_pool(name="psum", bufs=1))
 
-        scale_table = keep.tile([P, T], U8, name="scale_table", tag="late", align_bytes=64)
+
+        scale_table = keep.tile([P, T], U8, name="scale_table", tag="w1_room", align_bytes=64)
         nc.vector.memset(scale_table[:].bitcast(I32), 0)
-        w2_raw = keep.tile([P, PACK * N], F32, name="w2_raw", tag="last", align_bytes=64)
+        w2_raw = keep.tile([P, PACK * N], F32, name="w2_raw", tag="st_room", align_bytes=64)
         w2_rows = w2.rearrange("(p j) c -> p (j c)", j=PACK)
-        for cols in (slice(0, 512), slice(512, LEAD)):
+        for cols in LEAD:
             nc.sync.dma_start(out=w2_raw[:, cols], in_=w2_rows[:, cols])
         offsets = keep.tile([P, S // 16], U16, name="offsets")
         nc.sync.dma_start(offsets[:], offs)
         nc.sync.dma_start(out=scale_table[0:P:8, :].bitcast(I32), in_=x_scales[0].bitcast(I32))
-        nc.sync.dma_start(out=w2_raw[:, LEAD:], in_=w2_rows[:, LEAD:])
-        word_table = keep.tile([P, T], U32, name="word_table", tag="rounded", align_bytes=64)
+        nc.sync.dma_start(out=w2_raw[:, LEAD[-1].stop :], in_=w2_rows[:, LEAD[-1].stop :])
+        word_table = keep.tile([P, T], U32, name="word_table", tag="rounded_room", align_bytes=64)
         nc.sync.dma_start(out=word_table[:].bitcast(I32), in_=x_words[0].rearrange("p c r -> p (c r)").bitcast(I32))
         x_scale = keep.tile([P, S], U8, name="x_scale", align_bytes=64)
         nc.vector.memset(x_scale[:].bitcast(I32), 0)
         identity = keep.tile([P, P], F32, name="identity")
         nc.vector.memset(identity[:], 0.0)
-        warm = keep.tile([P, 1], F32, name="warm")
-        nc.scalar.activation(warm[:], identity[:, 0:1], ACT.Tanh)
         make_identity(nc, identity[:], nomemset=True)
 
         picked_scales = keep.tile([P, S], U8, name="picked_scales", align_bytes=64)
@@ -57,60 +56,60 @@ def tile_picked_phcell_none_po_kernel(tc, x_words, x_scales, w1, w2, st, offs, o
         for i in range(4):
             nc.sync.dma_start(out=x_scale[i:P:32, :].bitcast(I32), in_=picked_scales[8 * i : P : 32, :].bitcast(I32))
 
-        w1_raw = keep.tile([P, PACK * N], F32, name="w1_raw", tag="late", align_bytes=64)
+        w1_raw = keep.tile([P, PACK * N], F32, name="w1_raw", tag="w1_room", align_bytes=64)
         nc.sync.dma_start(out=w1_raw[:], in_=w1.rearrange("(p j) c -> p (j c)", j=PACK))
-        def round_weight(grouped, raw, rows):
-            dst = grouped[:].rearrange("p (t m j) -> p m t j", t=PACK, j=PACK)
-            src = raw.rearrange("p (j m t) -> p m t j", j=PACK, t=PACK)
-            nc.scalar.activation(dst[:, :rows], src[:, :rows], ACT.Copy)
-            nc.vector.tensor_copy(dst[:, rows:], src[:, rows:])
 
-        w2_bf = keep.tile([P, PACK * N], BF16, name="w2_bf", tag="picked", align_bytes=64)
-        round_weight(w2_bf, w2_raw[:], SCALAR_ROWS)
-        state = keep.tile([P, PACK * S], F32, name="state", tag="last", align_bytes=64)
+        def dealt(rounded, raw):
+            return rounded[:].rearrange("p (t m j) -> p m j t", t=PACK, j=PACK), raw[:].rearrange("p (j m t) -> p m j t", j=PACK, t=PACK)
+
+        w2_bf = keep.tile([P, PACK * N], BF16, name="w2_bf", tag="picked_room", align_bytes=64)
+        nc.vector.tensor_copy(*dealt(w2_bf, w2_raw))
+        state = keep.tile([P, PACK * S], F32, name="state", tag="st_room", align_bytes=64)
         st_rows = st.rearrange("(p t) j -> p (t j)", t=PACK)
-        for h in range(2):
-            nc.sync.dma_start(out=state[:, 2 * S * h : 2 * S * (h + 1)], in_=st_rows[:, 2 * S * h : 2 * S * (h + 1)])
+        for pair in PAIRS:
+            nc.sync.dma_start(out=state[:, pair.start * S : pair.stop * S], in_=st_rows[:, pair.start * S : pair.stop * S])
         state_t = state[:].rearrange("p (t j) -> p t j", t=PACK)
 
         w2_codes = keep.tile([P, N], U32, name="w2_codes", align_bytes=64)
         w2_scale = keep.tile([P, N], U8, name="w2_scale", align_bytes=64)
-        for u in range(2):
-            nc.vector.quantize_mx(out=w2_codes[:, u * HALF : (u + 1) * HALF].bitcast(FP8X4), scales=w2_scale[:, u * HALF : (u + 1) * HALF], in_=w2_bf[:, u * 1024 : (u + 1) * 1024])
-        x_codes = keep.tile([P, S], U32, name="x_codes", tag="picked", align_bytes=64)
+        nc.vector.quantize_mx(out=w2_codes[:].bitcast(FP8X4), scales=w2_scale[:], in_=w2_bf[:])
+        x_codes = keep.tile([P, S], U32, name="x_codes", tag="picked_room", align_bytes=64)
         for h in range(2):
             nc.vector.tensor_copy(x_codes[:, h * HALF : (h + 1) * HALF], word_table[:].indirect(offsets[:, h * HALF // 16 : (h + 1) * HALF // 16]))
-        w1_bf = keep.tile([P, PACK * N], BF16, name="w1_bf", tag="rounded", align_bytes=64)
-        round_weight(w1_bf, w1_raw[:], SCALAR_ROWS)
+        w1_bf = keep.tile([P, PACK * N], BF16, name="w1_bf", tag="rounded_room", align_bytes=64)
+        dst, src = dealt(w1_bf, w1_raw)
+        nc.scalar.activation(dst[:, :SCALAR_GROUPS], src[:, :SCALAR_GROUPS], ACT.Copy)
+        nc.vector.tensor_copy(dst[:, SCALAR_GROUPS:], src[:, SCALAR_GROUPS:])
         w1_codes = keep.tile([P, N], U32, name="w1_codes", align_bytes=64)
         w1_scale = keep.tile([P, N], U8, name="w1_scale", align_bytes=64)
         nc.vector.quantize_mx(out=w1_codes[:].bitcast(FP8X4), scales=w1_scale[:], in_=w1_bf[:])
 
-        def product(codes, scales, h, u, bank_tag, result, scale):
+        def minus_new(h, u, result):
             places = slice(h * HALF, (h + 1) * HALF)
-            bank = psum.tile([P, 2, HALF], F32, name=f"{bank_tag}_{h}", tag=bank_tag)
+            bank = psum.tile([P, 2, HALF], F32, name=f"new_bank{2 * h + u}")
             for i in range(2):
                 cols = slice((2 * u + i) * P, (2 * u + i + 1) * P)
-                nc.tensor.matmul_mx(out=bank[:, i, :], lhsT=codes[:, cols].bitcast(FP8X4), lhsT_scale=scales[:, cols], rhs=x_codes[:, places].bitcast(FP8X4), rhs_scale=x_scale[:, places], start=True, stop=True)
-            nc.scalar.activation(result, bank[:], ACT.Tanh, scale=scale)
+                nc.tensor.matmul_mx(out=bank[:, i, :], lhsT=w2_codes[:, cols].bitcast(FP8X4), lhsT_scale=w2_scale[:, cols], rhs=x_codes[:, places].bitcast(FP8X4), rhs_scale=x_scale[:, places], start=True, stop=True)
+            nc.scalar.activation(result, bank[:], ACT.Tanh, scale=-1.0)
 
-        chunks = [slice(q * CHUNK, (q + 1) * CHUNK) for q in range(4)]
-        early = keep.tile([P, 2, HALF], F32, name="early")
-        minus_first = (early[:], w1_raw[:, :S].rearrange("p (i j) -> p i j", i=2))
-        minus_second = w1_raw[:, S : 3 * S].rearrange("p (t j) -> p t j", t=PACK)
+        chunks = [slice(q * CHUNK, (q + 1) * CHUNK) for q in range(S // CHUNK)]
+        n_early = keep.tile([P, 2, HALF], F32, name="n_early")
+        n_first = (n_early[:], w1_raw[:, :S].rearrange("p (i j) -> p i j", i=2))
+        n_second = w1_raw[:, S : 3 * S].rearrange("p (t j) -> p t j", t=PACK)
         for u in range(2):
-            product(w2_codes, w2_scale, 0, u, f"new_bank{u}", minus_first[u], -1.0)
+            minus_new(0, u, n_first[u])
         for u in range(2):
-            product(w2_codes, w2_scale, 1, u, f"new_bank{2 + u}", minus_second[:, PAIRS[u], :], -1.0)
-        diffs = keep.tile([P, 3 * PACK * CHUNK], F32, name="diffs", tag="rounded", align_bytes=64)
-        diff_first = diffs[:, : PACK * HALF].rearrange("p (t j) -> p t j", t=PACK)
-        diff_third = diffs[:, PACK * HALF :].rearrange("p (t j) -> p t j", t=PACK)
-        for u in range(2):
-            nc.vector.tensor_tensor(diff_first[:, PAIRS[u], :], minus_first[u], state_t[:, PAIRS[u], :HALF], ALU.add)
-        nc.vector.tensor_tensor(diff_third, minus_second[:, :, :CHUNK], state_t[:, :, chunks[2]], ALU.add)
-        diff = (diff_first[:, :, chunks[0]], diff_first[:, :, chunks[1]], diff_third)
+            minus_new(1, u, n_second[:, PAIRS[u], :])
 
-        def gate_product(q):
+        sums = keep.tile([P, 3 * PACK * CHUNK], F32, name="sums", tag="rounded_room", align_bytes=64)
+        sum_first = sums[:, : PACK * HALF].rearrange("p (t j) -> p t j", t=PACK)
+        sum_third = sums[:, PACK * HALF :].rearrange("p (t j) -> p t j", t=PACK)
+        for u in range(2):
+            nc.vector.tensor_tensor(sum_first[:, PAIRS[u], :], n_first[u], state_t[:, PAIRS[u], :HALF], ALU.add)
+        nc.vector.tensor_tensor(sum_third, n_second[:, :, :CHUNK], state_t[:, :, chunks[2]], ALU.add)
+        chunk_sum = (sum_first[:, :, chunks[0]], sum_first[:, :, chunks[1]], sum_third)
+
+        def gate_of(q):
             bank = psum.tile([P, PACK, CHUNK], F32, name=f"gate_bank{q}")
             for t in range(PACK):
                 cols = slice(t * P, (t + 1) * P)
@@ -119,63 +118,59 @@ def tile_picked_phcell_none_po_kernel(tc, x_words, x_scales, w1, w2, st, offs, o
             nc.scalar.activation(gate[:], bank[:], ACT.Tanh, scale=0.5)
             return gate
 
-        gates = [gate_product(q) for q in range(2)]
-        bank = psum.tile([P, N], F32, name="turned_gate_bank")
-        nc.tensor.matmul_mx(out=bank[:], lhsT=x_codes[:, chunks[3]].bitcast(FP8X4), lhsT_scale=x_scale[:, chunks[3]], rhs=w1_codes[:].bitcast(FP8X4), rhs_scale=w1_scale[:], start=True, stop=True)
+        gates = [gate_of(0), gate_of(1)]
+        turned_bank = psum.tile([P, N], F32, name="turned_bank")
+        nc.tensor.matmul_mx(out=turned_bank[:], lhsT=x_codes[:, chunks[3]].bitcast(FP8X4), lhsT_scale=x_scale[:, chunks[3]], rhs=w1_codes[:].bitcast(FP8X4), rhs_scale=w1_scale[:], start=True, stop=True)
         turned_gate = keep.tile([P, N], F32, name="turned_gate")
-        nc.scalar.activation(turned_gate[:], bank[:], ACT.Tanh, scale=0.5)
-        turned_diff = psum.tile([P, N], F32, name="turned_diff", tag="new_bank1")
+        nc.scalar.activation(turned_gate[:], turned_bank[:], ACT.Tanh, scale=0.5)
+        turned_sum = psum.tile([P, N], F32, name="turned_sum", tag="new_bank1")
         for t in range(PACK):
             cols = slice(t * P, (t + 1) * P)
-            nc.tensor.matmul(turned_diff[:, cols], lhsT=state_t[:, t, chunks[3]], rhs=identity[:], is_transpose=True, start=True, stop=False)
-            nc.tensor.matmul(turned_diff[:, cols], lhsT=minus_second[:, t, CHUNK:], rhs=identity[:], is_transpose=True, start=False, stop=True)
-        gates.append(gate_product(2))
+            nc.tensor.matmul(turned_sum[:, cols], lhsT=state_t[:, t, chunks[3]], rhs=identity[:], is_transpose=True, start=True, stop=False)
+            nc.tensor.matmul(turned_sum[:, cols], lhsT=n_second[:, t, CHUNK:], rhs=identity[:], is_transpose=True, start=False, stop=True)
+        gates.append(gate_of(2))
 
         out_rows = out_0.rearrange("(p t) j -> p t j", t=PACK)
         out_words = out_1[0].rearrange("p c r -> p (c r)").bitcast(I32)
         y_scale = keep.tile([P, S], U8, name="y_scale", align_bytes=64)
-        y_codes = [keep.tile([P, HALF], U32, name=f"y_codes{u}", align_bytes=64) for u in range(2)]
-        y_bf = [keep.tile([P, PACK * HALF], BF16, name=f"y_bf{u}", align_bytes=64) for u in range(2)]
+        y_codes = [keep.tile([P, HALF], U32, name=f"y_codes{h}", align_bytes=64) for h in range(2)]
+        y_bf = [keep.tile([P, PACK * HALF], BF16, name=f"y_bf{h}", align_bytes=64) for h in range(2)]
 
-        def finish(step, lo, hi):
-            h, at = divmod(lo, HALF)
-            y = keep.tile([P, PACK, hi - lo], F32, name=f"y{lo}")
-            nc.vector.scalar_tensor_tensor(y[:], step, -0.5, state_t[:, :, lo:hi], ALU.mult, ALU.add)
-            nc.sync.dma_start(out=out_rows[:, :, lo:hi], in_=y[:])
-            dst = y_bf[h][:, PACK * at : PACK * (at + hi - lo)].rearrange("p (c i t) -> p c t i", i=4, t=PACK)
-            return dst, y[:].rearrange("p t (c i) -> p c t i", i=4)
+        def step_of(q):
+            step = keep.tile([P, PACK, CHUNK], F32, name=f"step{q}")
+            nc.vector.scalar_tensor_tensor(step[:], gates[q][:], 1.0, chunk_sum[q], ALU.add, ALU.mult)
+            return step
+
+        def finish(step, q):
+            h, at = divmod(q * CHUNK, HALF)
+            y = keep.tile([P, PACK, CHUNK], F32, name=f"y{q}")
+            nc.vector.scalar_tensor_tensor(y[:], step[:], -0.5, state_t[:, :, chunks[q]], ALU.mult, ALU.add)
+            nc.sync.dma_start(out=out_rows[:, :, chunks[q]], in_=y[:])
+            rounded = y_bf[h][:, PACK * at : PACK * (at + CHUNK)].rearrange("p (c i t) -> p c t i", i=4, t=PACK)
+            return rounded, y[:].rearrange("p t (c i) -> p c t i", i=4)
 
         def pack(lo, hi):
             h, at = divmod(lo, HALF)
             nc.vector.quantize_mx(out=y_codes[h][:, at : at + hi - lo].bitcast(FP8X4), scales=y_scale[:, lo:hi], in_=y_bf[h][:, PACK * at : PACK * (at + hi - lo)])
 
-        def mul(q):
-            step = keep.tile([P, PACK, CHUNK], F32, name=f"step{q}")
-            nc.vector.scalar_tensor_tensor(step[:], gates[q][:], 1.0, diff[q], ALU.add, ALU.mult)
-            return step
-
-        def finish_and_round(step, q):
-            dst, src = finish(step, chunks[q].start, chunks[q].stop)
-            nc.scalar.activation(dst, src, ACT.Copy)
-
-        steps = [mul(0), mul(1)]
-        finish_and_round(steps[0][:], 0)
+        steps = [step_of(0), step_of(1)]
+        nc.scalar.activation(*finish(steps[0], 0), ACT.Copy)
         turned_step = keep.tile([P, N], F32, name="turned_step")
-        nc.vector.scalar_tensor_tensor(turned_step[:], turned_gate[:], 1.0, turned_diff[:], ALU.add, ALU.mult)
-        back = psum.tile([P, PACK, CHUNK], F32, name="back", tag="new_bank3")
+        nc.vector.scalar_tensor_tensor(turned_step[:], turned_gate[:], 1.0, turned_sum[:], ALU.add, ALU.mult)
+        step_back = psum.tile([P, PACK, CHUNK], F32, name="step_back", tag="new_bank3")
         for t in range(PACK):
-            nc.tensor.transpose(back[:, t, :], turned_step[:, t * P : (t + 1) * P], identity[:])
-        finish_and_round(steps[1][:], 1)
-        steps.append(mul(2))
-        finish_and_round(back[:], 3)
-        dst, src = finish(steps[2][:], chunks[2].start, chunks[2].stop)
-        nc.scalar.activation(dst[:, :LAST_SHARE], src[:, :LAST_SHARE], ACT.Copy)
+            nc.tensor.transpose(step_back[:, t, :], turned_step[:, t * P : (t + 1) * P], identity[:])
+        nc.scalar.activation(*finish(steps[1], 1), ACT.Copy)
+        steps.append(step_of(2))
+        nc.scalar.activation(*finish(step_back, 3), ACT.Copy)
+        dst, src = finish(steps[2], 2)
+        nc.scalar.activation(dst[:, :SCALAR_LAST_GROUPS], src[:, :SCALAR_LAST_GROUPS], ACT.Copy)
         pack(0, HALF)
         nc.sync.dma_start(out=out_words[:, :HALF], in_=y_codes[0][:].bitcast(I32))
-        nc.vector.tensor_copy(dst[:, LAST_SHARE:], src[:, LAST_SHARE:])
+        nc.vector.tensor_copy(dst[:, SCALAR_LAST_GROUPS:], src[:, SCALAR_LAST_GROUPS:])
         pack(chunks[3].start, chunks[3].stop)
         pack(chunks[2].start, chunks[2].stop)
         nc.sync.dma_start(out=out_words[:, HALF:], in_=y_codes[1][:].bitcast(I32))
         for quad in range(4):
-            eng = nc.scalar if quad % 2 else nc.sync
-            eng.dma_start(out=out_2[0, 4 * quad : 4 * quad + 4, :].bitcast(I32), in_=y_scale[32 * quad : 32 * quad + 4, :].bitcast(I32))
+            queue = nc.scalar if quad % 2 else nc.sync
+            queue.dma_start(out=out_2[0, 4 * quad : 4 * quad + 4, :].bitcast(I32), in_=y_scale[32 * quad : 32 * quad + 4, :].bitcast(I32))

@@ -22,14 +22,14 @@ HALF = S // 2
 CHUNK = 128
 PAIRS = (slice(0, 2), slice(2, 4))
 LEAD = (slice(0, 512), slice(512, 768))
-SCALAR_GROUPS = 44
-SCALAR_LAST_GROUPS = 8
+SCALAR_LAST_GROUPS = 20
 
 
 def tile_picked_phcell_none_po_kernel(tc, x_words, x_scales, w1, w2, st, offs, out_0, out_1, out_2):
     nc = tc.nc
     with ExitStack() as ctx:
         keep = ctx.enter_context(tc.tile_pool(name="keep", bufs=1))
+        shared = ctx.enter_context(tc.tile_pool(name="shared", bufs=1))
         psum = ctx.enter_context(tc.psum_pool(name="psum", bufs=1))
 
 
@@ -43,7 +43,7 @@ def tile_picked_phcell_none_po_kernel(tc, x_words, x_scales, w1, w2, st, offs, o
         nc.sync.dma_start(offsets[:], offs)
         nc.sync.dma_start(out=scale_table[0:P:8, :].bitcast(I32), in_=x_scales[0].bitcast(I32))
         nc.sync.dma_start(out=w2_raw[:, LEAD[-1].stop :], in_=w2_rows[:, LEAD[-1].stop :])
-        word_table = keep.tile([P, T], U32, name="word_table", tag="rounded_room", align_bytes=64)
+        word_table = shared.tile([P, T], U32, name="word_table", offset=0, align_bytes=64)
         nc.sync.dma_start(out=word_table[:].bitcast(I32), in_=x_words[0].rearrange("p c r -> p (c r)").bitcast(I32))
         x_scale = keep.tile([P, S], U8, name="x_scale", align_bytes=64)
         nc.vector.memset(x_scale[:].bitcast(I32), 0)
@@ -56,19 +56,23 @@ def tile_picked_phcell_none_po_kernel(tc, x_words, x_scales, w1, w2, st, offs, o
         for i in range(4):
             nc.sync.dma_start(out=x_scale[i:P:32, :].bitcast(I32), in_=picked_scales[8 * i : P : 32, :].bitcast(I32))
 
-        w1_raw = keep.tile([P, PACK * N], F32, name="w1_raw", tag="w1_room", align_bytes=64)
-        nc.sync.dma_start(out=w1_raw[:], in_=w1.rearrange("(p j) c -> p (j c)", j=PACK))
+        w1_tile = keep.tile([P, PACK * N], F32, name="w1_tile", tag="w1_room", align_bytes=64)
+        w1_raw = w1_tile[:]
+        w1_rows = w1.rearrange("(p j) c -> p (j c)", j=PACK)
+        for pair in PAIRS:
+            nc.sync.dma_start(out=w1_raw[:, pair.start * N : pair.stop * N], in_=w1_rows[:, pair.start * N : pair.stop * N])
 
         def dealt(rounded, raw):
-            return rounded[:].rearrange("p (t m j) -> p m j t", t=PACK, j=PACK), raw[:].rearrange("p (j m t) -> p m j t", j=PACK, t=PACK)
+            return rounded[:].rearrange("p (t m j) -> p m j t", t=PACK, j=PACK), raw.rearrange("p (j m t) -> p m j t", j=PACK, t=PACK)
 
         w2_bf = keep.tile([P, PACK * N], BF16, name="w2_bf", tag="picked_room", align_bytes=64)
-        nc.vector.tensor_copy(*dealt(w2_bf, w2_raw))
-        state = keep.tile([P, PACK * S], F32, name="state", tag="st_room", align_bytes=64)
+        nc.vector.tensor_copy(*dealt(w2_bf, w2_raw[:]))
+        state_room = keep.tile([P, (PACK + 2) * S], F32, name="state_room", tag="st_room", align_bytes=64)
+        state = state_room[:, : PACK * S]
         st_rows = st.rearrange("(p t) j -> p (t j)", t=PACK)
         for pair in PAIRS:
             nc.sync.dma_start(out=state[:, pair.start * S : pair.stop * S], in_=st_rows[:, pair.start * S : pair.stop * S])
-        state_t = state[:].rearrange("p (t j) -> p t j", t=PACK)
+        state_t = state.rearrange("p (t j) -> p t j", t=PACK)
 
         w2_codes = keep.tile([P, N], U32, name="w2_codes", align_bytes=64)
         w2_scale = keep.tile([P, N], U8, name="w2_scale", align_bytes=64)
@@ -76,101 +80,124 @@ def tile_picked_phcell_none_po_kernel(tc, x_words, x_scales, w1, w2, st, offs, o
         x_codes = keep.tile([P, S], U32, name="x_codes", tag="picked_room", align_bytes=64)
         for h in range(2):
             nc.vector.tensor_copy(x_codes[:, h * HALF : (h + 1) * HALF], word_table[:].indirect(offsets[:, h * HALF // 16 : (h + 1) * HALF // 16]))
-        w1_bf = keep.tile([P, PACK * N], BF16, name="w1_bf", tag="rounded_room", align_bytes=64)
-        dst, src = dealt(w1_bf, w1_raw)
-        nc.scalar.activation(dst[:, :SCALAR_GROUPS], src[:, :SCALAR_GROUPS], ACT.Copy)
-        nc.vector.tensor_copy(dst[:, SCALAR_GROUPS:], src[:, SCALAR_GROUPS:])
-        w1_codes = keep.tile([P, N], U32, name="w1_codes", align_bytes=64)
-        w1_scale = keep.tile([P, N], U8, name="w1_scale", align_bytes=64)
-        nc.vector.quantize_mx(out=w1_codes[:].bitcast(FP8X4), scales=w1_scale[:], in_=w1_bf[:])
+        w1_bf = [shared.tile([P, PACK * HALF], BF16, name=f"w1_bf{u}", offset=u * 4 * S, align_bytes=64) for u in range(2)]
+        src = w1_raw.rearrange("p (j m t) -> p m j t", j=PACK, t=PACK)
+        dst = [w1_bf[u][:].rearrange("p (t m j) -> p m j t", t=2, j=PACK) for u in range(2)]
+        w1_codes = [keep.tile([P, HALF], U32, name=f"w1_codes{u}", align_bytes=64) for u in range(2)]
+        w1_scale = [keep.tile([P, HALF], U8, name=f"w1_scale{u}", align_bytes=64) for u in range(2)]
+        for rows in PAIRS:
+            for u in range(2):
+                nc.vector.tensor_copy(dst[u][:, :, rows], src[:, :, rows, PAIRS[u]])
+        for u in range(2):
+            nc.vector.quantize_mx(out=w1_codes[u][:].bitcast(FP8X4), scales=w1_scale[u][:], in_=w1_bf[u][:])
 
-        def minus_new(h, u, result):
-            places = slice(h * HALF, (h + 1) * HALF)
-            bank = psum.tile([P, 2, HALF], F32, name=f"new_bank{2 * h + u}")
+        halves = [slice(h * HALF, (h + 1) * HALF) for h in range(2)]
+
+        def new_of(u, h, result, func, scale):
+            bank = psum.tile([P, 2, HALF], F32, name=f"new_bank{u}{h}")
             for i in range(2):
                 cols = slice((2 * u + i) * P, (2 * u + i + 1) * P)
-                nc.tensor.matmul_mx(out=bank[:, i, :], lhsT=w2_codes[:, cols].bitcast(FP8X4), lhsT_scale=w2_scale[:, cols], rhs=x_codes[:, places].bitcast(FP8X4), rhs_scale=x_scale[:, places], start=True, stop=True)
-            nc.scalar.activation(result, bank[:], ACT.Tanh, scale=-1.0)
+                nc.tensor.matmul_mx(out=bank[:, i, :], lhsT=w2_codes[:, cols].bitcast(FP8X4), lhsT_scale=w2_scale[:, cols], rhs=x_codes[:, halves[h]].bitcast(FP8X4), rhs_scale=x_scale[:, halves[h]], start=True, stop=True)
+            nc.scalar.activation(result, bank[:], func, scale=scale)
 
-        chunks = [slice(q * CHUNK, (q + 1) * CHUNK) for q in range(S // CHUNK)]
-        n_early = keep.tile([P, 2, HALF], F32, name="n_early")
-        n_first = (n_early[:], w1_raw[:, :S].rearrange("p (i j) -> p i j", i=2))
-        n_second = w1_raw[:, S : 3 * S].rearrange("p (t j) -> p t j", t=PACK)
-        for u in range(2):
-            minus_new(0, u, n_first[u])
-        for u in range(2):
-            minus_new(1, u, n_second[:, PAIRS[u], :])
+        s_tile = keep.tile([P, 2, 2, HALF], F32, name="s_tile")
+        s_by_half = s_tile[:]
+        n_tile = keep.tile([P, 2, 2, HALF], F32, name="n_tile")
+        n_turn = (n_tile[:, 0], n_tile[:, 1])
+        new_of(0, 0, s_by_half[:, 0], ACT.Sigmoid, -2.0)
+        for h in range(2):
+            new_of(1, h, n_turn[h], ACT.Tanh, -1.0)
+        new_of(0, 1, s_by_half[:, 1], ACT.Sigmoid, -2.0)
 
-        sums = keep.tile([P, 3 * PACK * CHUNK], F32, name="sums", tag="rounded_room", align_bytes=64)
-        sum_first = sums[:, : PACK * HALF].rearrange("p (t j) -> p t j", t=PACK)
-        sum_third = sums[:, PACK * HALF :].rearrange("p (t j) -> p t j", t=PACK)
-        for u in range(2):
-            nc.vector.tensor_tensor(sum_first[:, PAIRS[u], :], n_first[u], state_t[:, PAIRS[u], :HALF], ALU.add)
-        nc.vector.tensor_tensor(sum_third, n_second[:, :, :CHUNK], state_t[:, :, chunks[2]], ALU.add)
-        chunk_sum = (sum_first[:, :, chunks[0]], sum_first[:, :, chunks[1]], sum_third)
+        turned_sum = [psum.tile([P, N], F32, name=f"turned_sum{h}", tag=f"new_bank1{h}") for h in range(2)]
+        blocks = [(c, i) for c in range(2) for i in range(2)]
 
-        def gate_of(q):
-            bank = psum.tile([P, PACK, CHUNK], F32, name=f"gate_bank{q}")
-            for t in range(PACK):
-                cols = slice(t * P, (t + 1) * P)
-                nc.tensor.matmul_mx(out=bank[:, t, :], lhsT=w1_codes[:, cols].bitcast(FP8X4), lhsT_scale=w1_scale[:, cols], rhs=x_codes[:, chunks[q]].bitcast(FP8X4), rhs_scale=x_scale[:, chunks[q]], start=True, stop=True)
-            gate = keep.tile([P, PACK, CHUNK], F32, name=f"gate{q}")
-            nc.scalar.activation(gate[:], bank[:], ACT.Tanh, scale=0.5)
-            return gate
+        late_identity = shared.tile([P, P], F32, name="late_identity", offset=4 * S, align_bytes=64)
+        nc.scalar.copy(late_identity[:], identity[:])
 
-        gates = [gate_of(0), gate_of(1)]
-        turned_bank = psum.tile([P, N], F32, name="turned_bank")
-        nc.tensor.matmul_mx(out=turned_bank[:], lhsT=x_codes[:, chunks[3]].bitcast(FP8X4), lhsT_scale=x_scale[:, chunks[3]], rhs=w1_codes[:].bitcast(FP8X4), rhs_scale=w1_scale[:], start=True, stop=True)
-        turned_gate = keep.tile([P, N], F32, name="turned_gate")
-        nc.scalar.activation(turned_gate[:], turned_bank[:], ACT.Tanh, scale=0.5)
-        turned_sum = psum.tile([P, N], F32, name="turned_sum", tag="new_bank1")
-        for t in range(PACK):
+        def turn_new(h):
+            for b, (c, i) in enumerate(blocks):
+                nc.tensor.matmul(turned_sum[h][:, b * P : (b + 1) * P], lhsT=n_turn[h][:, i, c * P : (c + 1) * P], rhs=(identity, late_identity)[h][:], is_transpose=True, start=(b == 0), stop=False)
+
+        def turn_state(h):
+            for b, (c, i) in enumerate(blocks):
+                at = h * HALF + c * P
+                nc.tensor.matmul(turned_sum[h][:, b * P : (b + 1) * P], lhsT=state_t[:, 2 + i, at : at + P], rhs=late_identity[:], is_transpose=True, start=False, stop=(b == 3))
+
+        turn_new(0)
+
+        sums = keep.tile([P, 2, 2, HALF], F32, name="sums")
+        for h in range(2):
+            nc.vector.scalar_tensor_tensor(sums[:, h], s_by_half[:, h], 2.0, state_t[:, PAIRS[0], halves[h]], ALU.mult, ALU.add)
+
+        gates = {}
+        for t in (1, 0):
+            bank = psum.tile([P, S], F32, name=f"gate_bank{t}")
             cols = slice(t * P, (t + 1) * P)
-            nc.tensor.matmul(turned_sum[:, cols], lhsT=state_t[:, t, chunks[3]], rhs=identity[:], is_transpose=True, start=True, stop=False)
-            nc.tensor.matmul(turned_sum[:, cols], lhsT=n_second[:, t, CHUNK:], rhs=identity[:], is_transpose=True, start=False, stop=True)
-        gates.append(gate_of(2))
+            nc.tensor.matmul_mx(out=bank[:], lhsT=w1_codes[0][:, cols].bitcast(FP8X4), lhsT_scale=w1_scale[0][:, cols], rhs=x_codes[:].bitcast(FP8X4), rhs_scale=x_scale[:], start=True, stop=True)
+            gate = keep.tile([P, S], F32, name=f"gate{t}")
+            nc.scalar.activation(gate[:], bank[:], ACT.Sigmoid)
+            gates[t] = gate
+        turned_gates = []
+        for h in range(2):
+            bank = psum.tile([P, N], F32, name=f"turned_bank{h}")
+            for c in range(2):
+                places = slice(h * HALF + c * P, h * HALF + (c + 1) * P)
+                nc.tensor.matmul_mx(out=bank[:, c * HALF : (c + 1) * HALF], lhsT=x_codes[:, places].bitcast(FP8X4), lhsT_scale=x_scale[:, places], rhs=w1_codes[1][:].bitcast(FP8X4), rhs_scale=w1_scale[1][:], start=True, stop=True)
+            gate = keep.tile([P, N], F32, name=f"turned_gate{h}")
+            nc.scalar.activation(gate[:], bank[:], ACT.Sigmoid)
+            turned_gates.append(gate)
+        turn_state(0)
+        turn_new(1)
+        turn_state(1)
 
         out_rows = out_0.rearrange("(p t) j -> p t j", t=PACK)
         out_words = out_1[0].rearrange("p c r -> p (c r)").bitcast(I32)
         y_scale = keep.tile([P, S], U8, name="y_scale", align_bytes=64)
         y_codes = [keep.tile([P, HALF], U32, name=f"y_codes{h}", align_bytes=64) for h in range(2)]
         y_bf = [keep.tile([P, PACK * HALF], BF16, name=f"y_bf{h}", align_bytes=64) for h in range(2)]
+        y_first = keep.tile([P, PACK, HALF], F32, name="y_first")
+        y = (y_first[:], state_room[:, 2 * S :].rearrange("p (t j) -> p t j", t=PACK)[:, :, :HALF])
 
-        def step_of(q):
-            step = keep.tile([P, PACK, CHUNK], F32, name=f"step{q}")
-            nc.vector.scalar_tensor_tensor(step[:], gates[q][:], 1.0, chunk_sum[q], ALU.add, ALU.mult)
-            return step
+        steps = keep.tile([P, 2, S], F32, name="steps")
+        def finish(engine, h, tiles, step):
+            engine.tensor_tensor(y[h][:, tiles, :], state_t[:, tiles, halves[h]], step, ALU.subtract)
+            nc.sync.dma_start(out=out_rows[:, tiles, halves[h]], in_=y[h][:, tiles, :])
 
-        def finish(step, q):
-            h, at = divmod(q * CHUNK, HALF)
-            y = keep.tile([P, PACK, CHUNK], F32, name=f"y{q}")
-            nc.vector.scalar_tensor_tensor(y[:], step[:], -0.5, state_t[:, :, chunks[q]], ALU.mult, ALU.add)
-            nc.sync.dma_start(out=out_rows[:, :, chunks[q]], in_=y[:])
-            rounded = y_bf[h][:, PACK * at : PACK * (at + CHUNK)].rearrange("p (c i t) -> p c t i", i=4, t=PACK)
-            return rounded, y[:].rearrange("p t (c i) -> p c t i", i=4)
+        for t in (1, 0):
+            nc.vector.scalar_tensor_tensor(steps[:, t, :].rearrange("p (h j) -> p h j", h=2), sums[:, :, t, :], -1.0, gates[t][:].rearrange("p (h j) -> p h j", h=2), ALU.add, ALU.mult)
+        backs = []
+        for h in range(2):
+            turned_step = keep.tile([P, N], F32, name=f"turned_step{h}")
+            nc.vector.tensor_tensor(turned_step[:], turned_gates[h][:], turned_sum[h][:], ALU.mult)
+            back = psum.tile([P, 2, HALF], F32, name=f"back{h}", tag=f"new_bank0{h}")
+            for b, (c, i) in enumerate(blocks):
+                nc.tensor.transpose(back[:, i, c * P : (c + 1) * P], turned_step[:, b * P : (b + 1) * P], identity[:])
+            backs.append(back)
+
+        def rounding(h):
+            return y_bf[h][:].rearrange("p (c i t) -> p c t i", i=4, t=PACK), y[h].rearrange("p t (c i) -> p c t i", i=4)
+
+        finish(nc.gpsimd, 0, PAIRS[0], steps[:, :, halves[0]])
+        finish(nc.vector, 0, PAIRS[1], backs[0][:])
+        finish(nc.vector, 1, PAIRS[1], backs[1][:])
+        finish(nc.vector, 1, PAIRS[0], steps[:, :, halves[1]])
 
         def pack(lo, hi):
             h, at = divmod(lo, HALF)
             nc.vector.quantize_mx(out=y_codes[h][:, at : at + hi - lo].bitcast(FP8X4), scales=y_scale[:, lo:hi], in_=y_bf[h][:, PACK * at : PACK * (at + hi - lo)])
 
-        steps = [step_of(0), step_of(1)]
-        nc.scalar.activation(*finish(steps[0], 0), ACT.Copy)
-        turned_step = keep.tile([P, N], F32, name="turned_step")
-        nc.vector.scalar_tensor_tensor(turned_step[:], turned_gate[:], 1.0, turned_sum[:], ALU.add, ALU.mult)
-        step_back = psum.tile([P, PACK, CHUNK], F32, name="step_back", tag="new_bank3")
-        for t in range(PACK):
-            nc.tensor.transpose(step_back[:, t, :], turned_step[:, t * P : (t + 1) * P], identity[:])
-        nc.scalar.activation(*finish(steps[1], 1), ACT.Copy)
-        steps.append(step_of(2))
-        nc.scalar.activation(*finish(step_back, 3), ACT.Copy)
-        dst, src = finish(steps[2], 2)
+        dst, src = rounding(0)
+        for c in range(2):
+            nc.scalar.activation(dst[:, 32 * c : 32 * c + 32], src[:, 32 * c : 32 * c + 32], ACT.Copy)
+        pack(0, CHUNK)
+        dst, src = rounding(1)
         nc.scalar.activation(dst[:, :SCALAR_LAST_GROUPS], src[:, :SCALAR_LAST_GROUPS], ACT.Copy)
-        pack(0, HALF)
-        nc.sync.dma_start(out=out_words[:, :HALF], in_=y_codes[0][:].bitcast(I32))
         nc.vector.tensor_copy(dst[:, SCALAR_LAST_GROUPS:], src[:, SCALAR_LAST_GROUPS:])
-        pack(chunks[3].start, chunks[3].stop)
-        pack(chunks[2].start, chunks[2].stop)
-        nc.sync.dma_start(out=out_words[:, HALF:], in_=y_codes[1][:].bitcast(I32))
+        pack(CHUNK, HALF)
+        nc.sync.dma_start(out=out_words[:, halves[0]], in_=y_codes[0][:].bitcast(I32))
+        pack(HALF, S)
+        nc.sync.dma_start(out=out_words[:, halves[1]], in_=y_codes[1][:].bitcast(I32))
         for quad in range(4):
             queue = nc.scalar if quad % 2 else nc.sync
             queue.dma_start(out=out_2[0, 4 * quad : 4 * quad + 4, :].bitcast(I32), in_=y_scale[32 * quad : 32 * quad + 4, :].bitcast(I32))

@@ -22,7 +22,6 @@ HALF = S // 2
 CHUNK = 128
 PAIRS = (slice(0, 2), slice(2, 4))
 LEAD = (slice(0, 512), slice(512, 768))
-SCALAR_LAST_GROUPS = 20
 
 
 def tile_picked_phcell_none_po_kernel(tc, x_words, x_scales, w1, w2, st, offs, out_0, out_1, out_2):
@@ -67,12 +66,11 @@ def tile_picked_phcell_none_po_kernel(tc, x_words, x_scales, w1, w2, st, offs, o
 
         w2_bf = keep.tile([P, PACK * N], BF16, name="w2_bf", tag="picked_room", align_bytes=64)
         nc.vector.tensor_copy(*dealt(w2_bf, w2_raw[:]))
-        state_room = keep.tile([P, (PACK + 2) * S], F32, name="state_room", tag="st_room", align_bytes=64)
-        state = state_room[:, : PACK * S]
+        state = keep.tile([P, PACK * S], F32, name="state", tag="st_room", align_bytes=64)
         st_rows = st.rearrange("(p t) j -> p (t j)", t=PACK)
         for pair in PAIRS:
             nc.sync.dma_start(out=state[:, pair.start * S : pair.stop * S], in_=st_rows[:, pair.start * S : pair.stop * S])
-        state_t = state.rearrange("p (t j) -> p t j", t=PACK)
+        state_t = state[:].rearrange("p (t j) -> p t j", t=PACK)
 
         w2_codes = keep.tile([P, N], U32, name="w2_codes", align_bytes=64)
         w2_scale = keep.tile([P, N], U8, name="w2_scale", align_bytes=64)
@@ -117,7 +115,7 @@ def tile_picked_phcell_none_po_kernel(tc, x_words, x_scales, w1, w2, st, offs, o
 
         def turn_new(h):
             for b, (c, i) in enumerate(blocks):
-                nc.tensor.matmul(turned_sum[h][:, b * P : (b + 1) * P], lhsT=n_turn[h][:, i, c * P : (c + 1) * P], rhs=(identity, late_identity)[h][:], is_transpose=True, start=(b == 0), stop=False)
+                nc.tensor.matmul(turned_sum[h][:, b * P : (b + 1) * P], lhsT=n_turn[h][:, i, c * P : (c + 1) * P], rhs=identity[:], is_transpose=True, start=(b == 0), stop=False)
 
         def turn_state(h):
             for b, (c, i) in enumerate(blocks):
@@ -125,30 +123,34 @@ def tile_picked_phcell_none_po_kernel(tc, x_words, x_scales, w1, w2, st, offs, o
                 nc.tensor.matmul(turned_sum[h][:, b * P : (b + 1) * P], lhsT=state_t[:, 2 + i, at : at + P], rhs=late_identity[:], is_transpose=True, start=False, stop=(b == 3))
 
         turn_new(0)
+        turn_new(1)
 
         sums = keep.tile([P, 2, 2, HALF], F32, name="sums")
         for h in range(2):
             nc.vector.scalar_tensor_tensor(sums[:, h], s_by_half[:, h], 2.0, state_t[:, PAIRS[0], halves[h]], ALU.mult, ALU.add)
 
-        gates = {}
-        for t in (1, 0):
-            bank = psum.tile([P, S], F32, name=f"gate_bank{t}")
-            cols = slice(t * P, (t + 1) * P)
-            nc.tensor.matmul_mx(out=bank[:], lhsT=w1_codes[0][:, cols].bitcast(FP8X4), lhsT_scale=w1_scale[0][:, cols], rhs=x_codes[:].bitcast(FP8X4), rhs_scale=x_scale[:], start=True, stop=True)
-            gate = keep.tile([P, S], F32, name=f"gate{t}")
+        def direct_gate(h):
+            bank = psum.tile([P, 2, HALF], F32, name=f"gate_bank{h}")
+            for t in range(2):
+                cols = slice(t * P, (t + 1) * P)
+                nc.tensor.matmul_mx(out=bank[:, t, :], lhsT=w1_codes[0][:, cols].bitcast(FP8X4), lhsT_scale=w1_scale[0][:, cols], rhs=x_codes[:, halves[h]].bitcast(FP8X4), rhs_scale=x_scale[:, halves[h]], start=True, stop=True)
+            gate = keep.tile([P, 2, HALF], F32, name=f"gate{h}")
             nc.scalar.activation(gate[:], bank[:], ACT.Sigmoid)
-            gates[t] = gate
-        turned_gates = []
-        for h in range(2):
+            return gate
+
+        def turned_gate(h):
             bank = psum.tile([P, N], F32, name=f"turned_bank{h}")
             for c in range(2):
                 places = slice(h * HALF + c * P, h * HALF + (c + 1) * P)
                 nc.tensor.matmul_mx(out=bank[:, c * HALF : (c + 1) * HALF], lhsT=x_codes[:, places].bitcast(FP8X4), lhsT_scale=x_scale[:, places], rhs=w1_codes[1][:].bitcast(FP8X4), rhs_scale=w1_scale[1][:], start=True, stop=True)
             gate = keep.tile([P, N], F32, name=f"turned_gate{h}")
             nc.scalar.activation(gate[:], bank[:], ACT.Sigmoid)
-            turned_gates.append(gate)
+            return gate
+
+        gates = [direct_gate(0)]
+        turned_gates = [turned_gate(h) for h in range(2)]
         turn_state(0)
-        turn_new(1)
+        gates.append(direct_gate(1))
         turn_state(1)
 
         out_rows = out_0.rearrange("(p t) j -> p t j", t=PACK)
@@ -156,47 +158,50 @@ def tile_picked_phcell_none_po_kernel(tc, x_words, x_scales, w1, w2, st, offs, o
         y_scale = keep.tile([P, S], U8, name="y_scale", align_bytes=64)
         y_codes = [keep.tile([P, HALF], U32, name=f"y_codes{h}", align_bytes=64) for h in range(2)]
         y_bf = [keep.tile([P, PACK * HALF], BF16, name=f"y_bf{h}", align_bytes=64) for h in range(2)]
-        y_first = keep.tile([P, PACK, HALF], F32, name="y_first")
-        y = (y_first[:], state_room[:, 2 * S :].rearrange("p (t j) -> p t j", t=PACK)[:, :, :HALF])
+        y = [keep.tile([P, PACK, HALF], F32, name=f"y{h}")[:] for h in range(2)]
 
-        steps = keep.tile([P, 2, S], F32, name="steps")
         def finish(engine, h, tiles, step):
             engine.tensor_tensor(y[h][:, tiles, :], state_t[:, tiles, halves[h]], step, ALU.subtract)
             nc.sync.dma_start(out=out_rows[:, tiles, halves[h]], in_=y[h][:, tiles, :])
 
-        for t in (1, 0):
-            nc.vector.scalar_tensor_tensor(steps[:, t, :].rearrange("p (h j) -> p h j", h=2), sums[:, :, t, :], -1.0, gates[t][:].rearrange("p (h j) -> p h j", h=2), ALU.add, ALU.mult)
-        backs = []
-        for h in range(2):
-            turned_step = keep.tile([P, N], F32, name=f"turned_step{h}")
-            nc.vector.tensor_tensor(turned_step[:], turned_gates[h][:], turned_sum[h][:], ALU.mult)
+        def direct_step(h):
+            step = keep.tile([P, 2, HALF], F32, name=f"step{h}", tag=("step0", "turned_step0")[h])
+            nc.vector.scalar_tensor_tensor(step[:], sums[:, h], -1.0, gates[h][:], ALU.add, ALU.mult)
+            return step
+
+        def turned_step(h):
+            step = keep.tile([P, N], F32, name=f"turned_step{h}")
+            nc.vector.tensor_tensor(step[:], turned_gates[h][:], turned_sum[h][:], ALU.mult)
             back = psum.tile([P, 2, HALF], F32, name=f"back{h}", tag=f"new_bank0{h}")
             for b, (c, i) in enumerate(blocks):
-                nc.tensor.transpose(back[:, i, c * P : (c + 1) * P], turned_step[:, b * P : (b + 1) * P], identity[:])
-            backs.append(back)
+                nc.tensor.transpose(back[:, i, c * P : (c + 1) * P], step[:, b * P : (b + 1) * P], identity[:])
+            return back
 
         def rounding(h):
             return y_bf[h][:].rearrange("p (c i t) -> p c t i", i=4, t=PACK), y[h].rearrange("p t (c i) -> p c t i", i=4)
 
-        finish(nc.gpsimd, 0, PAIRS[0], steps[:, :, halves[0]])
+        finish(nc.gpsimd, 0, PAIRS[0], direct_step(0)[:])
+        backs = [turned_step(h) for h in range(2)]
         finish(nc.vector, 0, PAIRS[1], backs[0][:])
+        last_step = direct_step(1)
         finish(nc.vector, 1, PAIRS[1], backs[1][:])
-        finish(nc.vector, 1, PAIRS[0], steps[:, :, halves[1]])
+        for c in range(2):
+            part = slice(c * CHUNK, (c + 1) * CHUNK)
+            nc.vector.tensor_tensor(y[1][:, PAIRS[0], part], state_t[:, PAIRS[0], halves[1]][:, :, part], last_step[:, :, part], ALU.subtract)
+        nc.sync.dma_start(out=out_rows[:, PAIRS[0], halves[1]], in_=y[1][:, PAIRS[0], :])
 
         def pack(lo, hi):
             h, at = divmod(lo, HALF)
             nc.vector.quantize_mx(out=y_codes[h][:, at : at + hi - lo].bitcast(FP8X4), scales=y_scale[:, lo:hi], in_=y_bf[h][:, PACK * at : PACK * (at + hi - lo)])
 
-        dst, src = rounding(0)
-        for c in range(2):
-            nc.scalar.activation(dst[:, 32 * c : 32 * c + 32], src[:, 32 * c : 32 * c + 32], ACT.Copy)
-        pack(0, CHUNK)
+        nc.scalar.activation(*rounding(0), ACT.Copy)
         dst, src = rounding(1)
-        nc.scalar.activation(dst[:, :SCALAR_LAST_GROUPS], src[:, :SCALAR_LAST_GROUPS], ACT.Copy)
-        nc.vector.tensor_copy(dst[:, SCALAR_LAST_GROUPS:], src[:, SCALAR_LAST_GROUPS:])
-        pack(CHUNK, HALF)
+        nc.scalar.activation(dst[:, :32], src[:, :32], ACT.Copy)
+        pack(0, HALF)
         nc.sync.dma_start(out=out_words[:, halves[0]], in_=y_codes[0][:].bitcast(I32))
-        pack(HALF, S)
+        nc.vector.tensor_copy(dst[:, 32:], src[:, 32:])
+        pack(HALF, HALF + CHUNK)
+        pack(HALF + CHUNK, S)
         nc.sync.dma_start(out=out_words[:, halves[1]], in_=y_codes[1][:].bitcast(I32))
         for quad in range(4):
             queue = nc.scalar if quad % 2 else nc.sync

@@ -115,7 +115,7 @@ def tile_picked_phcell_none_po_kernel(tc, x_words, x_scales, w1, w2, st, offs, o
 
         def turn_new(h):
             for b, (c, i) in enumerate(blocks):
-                nc.tensor.matmul(turned_sum[h][:, b * P : (b + 1) * P], lhsT=n_turn[h][:, i, c * P : (c + 1) * P], rhs=identity[:], is_transpose=True, start=(b == 0), stop=False)
+                nc.tensor.matmul(turned_sum[h][:, b * P : (b + 1) * P], lhsT=n_turn[h][:, i, c * P : (c + 1) * P], rhs=(identity, late_identity)[h][:], is_transpose=True, start=(b == 0), stop=False)
 
         def turn_state(h):
             for b, (c, i) in enumerate(blocks):
@@ -123,7 +123,6 @@ def tile_picked_phcell_none_po_kernel(tc, x_words, x_scales, w1, w2, st, offs, o
                 nc.tensor.matmul(turned_sum[h][:, b * P : (b + 1) * P], lhsT=state_t[:, 2 + i, at : at + P], rhs=late_identity[:], is_transpose=True, start=False, stop=(b == 3))
 
         turn_new(0)
-        turn_new(1)
 
         sums = keep.tile([P, 2, 2, HALF], F32, name="sums")
         for h in range(2):
@@ -149,8 +148,9 @@ def tile_picked_phcell_none_po_kernel(tc, x_words, x_scales, w1, w2, st, offs, o
 
         gates = [direct_gate(0)]
         turned_gates = [turned_gate(h) for h in range(2)]
-        turn_state(0)
         gates.append(direct_gate(1))
+        turn_state(0)
+        turn_new(1)
         turn_state(1)
 
         out_rows = out_0.rearrange("(p t) j -> p t j", t=PACK)

@@ -21,7 +21,7 @@ PACK = 4
 HALF = S // 2
 CHUNK = 128
 PAIRS = (slice(0, 2), slice(2, 4))
-LEAD = (slice(0, 512), slice(512, 768))
+LEAD = (slice(0, 768),)
 
 
 def tile_picked_phcell_none_po_kernel(tc, x_words, x_scales, w1, w2, st, offs, out_0, out_1, out_2):
@@ -52,14 +52,14 @@ def tile_picked_phcell_none_po_kernel(tc, x_words, x_scales, w1, w2, st, offs, o
 
         picked_scales = keep.tile([P, S], U8, name="picked_scales", align_bytes=64)
         nc.vector.tensor_copy(picked_scales[:], scale_table[:].indirect(offsets[:]))
-        for i in range(4):
-            nc.sync.dma_start(out=x_scale[i:P:32, :].bitcast(I32), in_=picked_scales[8 * i : P : 32, :].bitcast(I32))
-
         w1_tile = keep.tile([P, PACK * N], F32, name="w1_tile", tag="w1_room", align_bytes=64)
         w1_raw = w1_tile[:]
         w1_rows = w1.rearrange("(p j) c -> p (j c)", j=PACK)
-        for pair in PAIRS:
-            nc.sync.dma_start(out=w1_raw[:, pair.start * N : pair.stop * N], in_=w1_rows[:, pair.start * N : pair.stop * N])
+        nc.sync.dma_start(out=w1_raw[:, :N], in_=w1_rows[:, :N])
+        for i in range(4):
+            nc.sync.dma_start(out=x_scale[i:P:32, :].bitcast(I32), in_=picked_scales[8 * i : P : 32, :].bitcast(I32))
+        for cols in (slice(N, 2 * N), slice(2 * N, 4 * N)):
+            nc.sync.dma_start(out=w1_raw[:, cols], in_=w1_rows[:, cols])
 
         def dealt(rounded, raw):
             return rounded[:].rearrange("p (t m j) -> p m j t", t=PACK, j=PACK), raw.rearrange("p (j m t) -> p m j t", j=PACK, t=PACK)
@@ -129,7 +129,7 @@ def tile_picked_phcell_none_po_kernel(tc, x_words, x_scales, w1, w2, st, offs, o
             nc.vector.scalar_tensor_tensor(sums[:, h], s_by_half[:, h], 2.0, state_t[:, PAIRS[0], halves[h]], ALU.mult, ALU.add)
 
         def direct_gate(h):
-            bank = psum.tile([P, 2, HALF], F32, name=f"gate_bank{h}")
+            bank = psum.tile([P, 2, HALF], F32, name=f"gate_bank{h}", tag=("gate_bank0", "turned_bank0")[h])
             for t in range(2):
                 cols = slice(t * P, (t + 1) * P)
                 nc.tensor.matmul_mx(out=bank[:, t, :], lhsT=w1_codes[0][:, cols].bitcast(FP8X4), lhsT_scale=w1_scale[0][:, cols], rhs=x_codes[:, halves[h]].bitcast(FP8X4), rhs_scale=x_scale[:, halves[h]], start=True, stop=True)
@@ -148,10 +148,10 @@ def tile_picked_phcell_none_po_kernel(tc, x_words, x_scales, w1, w2, st, offs, o
 
         gates = [direct_gate(0)]
         turned_gates = [turned_gate(h) for h in range(2)]
-        gates.append(direct_gate(1))
         turn_state(0)
         turn_new(1)
         turn_state(1)
+        gates.append(direct_gate(1))
 
         out_rows = out_0.rearrange("(p t) j -> p t j", t=PACK)
         out_words = out_1[0].rearrange("p c r -> p (c r)").bitcast(I32)
@@ -171,7 +171,8 @@ def tile_picked_phcell_none_po_kernel(tc, x_words, x_scales, w1, w2, st, offs, o
 
         def turned_step(h):
             step = keep.tile([P, N], F32, name=f"turned_step{h}")
-            nc.vector.tensor_tensor(step[:], turned_gates[h][:], turned_sum[h][:], ALU.mult)
+            for half in halves:
+                nc.vector.tensor_tensor(step[:, half], turned_gates[h][:, half], turned_sum[h][:, half], ALU.mult)
             back = psum.tile([P, 2, HALF], F32, name=f"back{h}", tag=f"new_bank0{h}")
             for b, (c, i) in enumerate(blocks):
                 nc.tensor.transpose(back[:, i, c * P : (c + 1) * P], step[:, b * P : (b + 1) * P], identity[:])

@@ -29,12 +29,13 @@ def tile_picked_phcell_none_po_kernel(tc, x_words, x_scales, w1, w2, st, offs, o
     with ExitStack() as ctx:
         keep = ctx.enter_context(tc.tile_pool(name="keep", bufs=1))
         shared = ctx.enter_context(tc.tile_pool(name="shared", bufs=1))
+        room = ctx.enter_context(tc.tile_pool(name="room", bufs=1))
         psum = ctx.enter_context(tc.psum_pool(name="psum", bufs=1))
 
 
         scale_table = keep.tile([P, T], U8, name="scale_table", tag="w1_room", align_bytes=64)
         nc.vector.memset(scale_table[:].bitcast(I32), 0)
-        w2_raw = keep.tile([P, PACK * N], F32, name="w2_raw", tag="st_room", align_bytes=64)
+        w2_raw = room.tile([P, PACK * N], F32, name="w2_raw", offset=0, align_bytes=64)
         w2_rows = w2.rearrange("(p j) c -> p (j c)", j=PACK)
         for cols in LEAD:
             nc.sync.dma_start(out=w2_raw[:, cols], in_=w2_rows[:, cols])
@@ -66,11 +67,14 @@ def tile_picked_phcell_none_po_kernel(tc, x_words, x_scales, w1, w2, st, offs, o
 
         w2_bf = keep.tile([P, PACK * N], BF16, name="w2_bf", tag="picked_room", align_bytes=64)
         nc.vector.tensor_copy(*dealt(w2_bf, w2_raw[:]))
-        state = keep.tile([P, PACK * S], F32, name="state", tag="st_room", align_bytes=64)
-        st_rows = st.rearrange("(p t) j -> p (t j)", t=PACK)
-        for pair in PAIRS:
-            nc.sync.dma_start(out=state[:, pair.start * S : pair.stop * S], in_=st_rows[:, pair.start * S : pair.stop * S])
-        state_t = state[:].rearrange("p (t j) -> p t j", t=PACK)
+        st_rows = st.rearrange("(p t) j -> p t j", t=PACK)
+        st_first = room.tile([P, 2, S - CHUNK], F32, name="st_first", offset=0, align_bytes=64)
+        st_last = room.tile([P, 2, CHUNK], F32, name="st_last", offset=8 * (S - CHUNK), align_bytes=64)
+        st_turn = room.tile([P, 2, S], F32, name="st_turn", offset=8 * S, align_bytes=64)
+        nc.sync.dma_start(out=st_first[:], in_=st_rows[:, PAIRS[0], : S - CHUNK])
+        nc.sync.dma_start(out=st_turn[:], in_=st_rows[:, PAIRS[1], :])
+        nc.sync.dma_start(out=st_last[:], in_=st_rows[:, PAIRS[0], S - CHUNK :])
+        st_quarter = (st_first[:, :, HALF:], st_last[:])
 
         w2_codes = keep.tile([P, N], U32, name="w2_codes", align_bytes=64)
         w2_scale = keep.tile([P, N], U8, name="w2_scale", align_bytes=64)
@@ -81,36 +85,36 @@ def tile_picked_phcell_none_po_kernel(tc, x_words, x_scales, w1, w2, st, offs, o
         w1_bf = [shared.tile([P, PACK * HALF], BF16, name=f"w1_bf{u}", offset=u * 4 * S, align_bytes=64) for u in range(2)]
         src = w1_raw.rearrange("p (j m t) -> p m j t", j=PACK, t=PACK)
         dst = [w1_bf[u][:].rearrange("p (t m j) -> p m j t", t=2, j=PACK) for u in range(2)]
-        w1_codes = [keep.tile([P, HALF], U32, name=f"w1_codes{u}", align_bytes=64) for u in range(2)]
-        w1_scale = [keep.tile([P, HALF], U8, name=f"w1_scale{u}", align_bytes=64) for u in range(2)]
+        w1_codes = [keep.tile([P, width], U32, name=f"w1_codes{u}", align_bytes=64) for u, width in enumerate((P, P, HALF))]
+        w1_scale = [keep.tile([P, width], U8, name=f"w1_scale{u}", align_bytes=64) for u, width in enumerate((P, P, HALF))]
         for rows in PAIRS:
             for u in range(2):
                 nc.vector.tensor_copy(dst[u][:, :, rows], src[:, :, rows, PAIRS[u]])
-        for u in range(2):
-            nc.vector.quantize_mx(out=w1_codes[u][:].bitcast(FP8X4), scales=w1_scale[u][:], in_=w1_bf[u][:])
+        for u, rounded in enumerate((w1_bf[0][:, : PACK * P], w1_bf[0][:, PACK * P :], w1_bf[1][:])):
+            nc.vector.quantize_mx(out=w1_codes[u][:].bitcast(FP8X4), scales=w1_scale[u][:], in_=rounded)
 
         halves = [slice(h * HALF, (h + 1) * HALF) for h in range(2)]
 
-        def new_of(u, h, result, func, scale):
-            bank = psum.tile([P, 2, HALF], F32, name=f"new_bank{u}{h}")
+        def new_of(u, places, tag, result, func, scale):
+            bank = psum.tile([P, 2, HALF], F32, name=f"new_{tag}", tag=tag)[:, :, : places.stop - places.start]
             for i in range(2):
                 cols = slice((2 * u + i) * P, (2 * u + i + 1) * P)
-                nc.tensor.matmul_mx(out=bank[:, i, :], lhsT=w2_codes[:, cols].bitcast(FP8X4), lhsT_scale=w2_scale[:, cols], rhs=x_codes[:, halves[h]].bitcast(FP8X4), rhs_scale=x_scale[:, halves[h]], start=True, stop=True)
-            nc.scalar.activation(result, bank[:], func, scale=scale)
+                nc.tensor.matmul_mx(out=bank[:, i, :], lhsT=w2_codes[:, cols].bitcast(FP8X4), lhsT_scale=w2_scale[:, cols], rhs=x_codes[:, places].bitcast(FP8X4), rhs_scale=x_scale[:, places], start=True, stop=True)
+            nc.scalar.activation(result, bank, func, scale=scale)
 
-        s_tile = keep.tile([P, 2, 2, HALF], F32, name="s_tile")
-        s_by_half = s_tile[:]
+        s_first = keep.tile([P, 2, HALF], F32, name="s_first")
+        n_direct = keep.tile([P, 2, HALF], F32, name="n_direct")
         n_tile = keep.tile([P, 2, 2, HALF], F32, name="n_tile")
         n_turn = (n_tile[:, 0], n_tile[:, 1])
-        new_of(0, 0, s_by_half[:, 0], ACT.Sigmoid, -2.0)
+        new_of(0, halves[0], "new_bank00", s_first[:], ACT.Sigmoid, -2.0)
         for h in range(2):
-            new_of(1, h, n_turn[h], ACT.Tanh, -1.0)
-        new_of(0, 1, s_by_half[:, 1], ACT.Sigmoid, -2.0)
+            new_of(1, halves[h], f"new_bank1{h}", n_turn[h], ACT.Tanh, -1.0)
+        new_of(0, halves[1], "new_bank01", n_direct[:], ACT.Tanh, -1.0)
 
         turned_sum = [psum.tile([P, N], F32, name=f"turned_sum{h}", tag=f"new_bank1{h}") for h in range(2)]
         blocks = [(c, i) for c in range(2) for i in range(2)]
 
-        late_identity = shared.tile([P, P], F32, name="late_identity", offset=4 * S, align_bytes=64)
+        late_identity = shared.tile([P, P], F32, name="late_identity", offset=0, align_bytes=64)
         nc.scalar.copy(late_identity[:], identity[:])
 
         def turn_new(h):
@@ -120,28 +124,35 @@ def tile_picked_phcell_none_po_kernel(tc, x_words, x_scales, w1, w2, st, offs, o
         def turn_state(h):
             for b, (c, i) in enumerate(blocks):
                 at = h * HALF + c * P
-                nc.tensor.matmul(turned_sum[h][:, b * P : (b + 1) * P], lhsT=state_t[:, 2 + i, at : at + P], rhs=late_identity[:], is_transpose=True, start=False, stop=(b == 3))
+                nc.tensor.matmul(turned_sum[h][:, b * P : (b + 1) * P], lhsT=st_turn[:, i, at : at + P], rhs=late_identity[:], is_transpose=True, start=False, stop=(b == 3))
 
         turn_new(0)
 
-        sums = keep.tile([P, 2, 2, HALF], F32, name="sums")
-        for h in range(2):
-            nc.vector.scalar_tensor_tensor(sums[:, h], s_by_half[:, h], 2.0, state_t[:, PAIRS[0], halves[h]], ALU.mult, ALU.add)
+        first_sum = keep.tile([P, 2, HALF], F32, name="first_sum")
+        nc.vector.scalar_tensor_tensor(first_sum[:], s_first[:], 2.0, st_first[:, :, :HALF], ALU.mult, ALU.add)
+        last_sum = [keep.tile([P, 2, CHUNK], F32, name="last_sum0")]
+        nc.vector.tensor_tensor(last_sum[0][:], st_quarter[0], n_direct[:, :, :CHUNK], ALU.add)
 
         def direct_gate(h):
-            bank = psum.tile([P, 2, HALF], F32, name=f"gate_bank{h}", tag=("gate_bank0", "turned_bank0")[h])
-            for t in range(2):
-                cols = slice(t * P, (t + 1) * P)
-                nc.tensor.matmul_mx(out=bank[:, t, :], lhsT=w1_codes[0][:, cols].bitcast(FP8X4), lhsT_scale=w1_scale[0][:, cols], rhs=x_codes[:, halves[h]].bitcast(FP8X4), rhs_scale=x_scale[:, halves[h]], start=True, stop=True)
             gate = keep.tile([P, 2, HALF], F32, name=f"gate{h}")
-            nc.scalar.activation(gate[:], bank[:], ACT.Sigmoid)
+            if h:
+                bank = psum.tile([P, 2, HALF], F32, name="last_gate_bank", tag="turned_bank0")
+                banks = [bank[:, t, :] for t in range(2)]
+            else:
+                banks = [psum.tile([P, N], F32, name=f"gate_bank{t}")[:, :HALF] for t in range(2)]
+            for t in range(2):
+                nc.tensor.matmul_mx(out=banks[t], lhsT=w1_codes[t][:].bitcast(FP8X4), lhsT_scale=w1_scale[t][:], rhs=x_codes[:, halves[h]].bitcast(FP8X4), rhs_scale=x_scale[:, halves[h]], start=True, stop=True)
+                if not h:
+                    nc.scalar.activation(gate[:, t, :], banks[t], ACT.Sigmoid)
+            if h:
+                nc.scalar.activation(gate[:], bank[:], ACT.Sigmoid)
             return gate
 
         def turned_gate(h):
             bank = psum.tile([P, N], F32, name=f"turned_bank{h}")
             for c in range(2):
                 places = slice(h * HALF + c * P, h * HALF + (c + 1) * P)
-                nc.tensor.matmul_mx(out=bank[:, c * HALF : (c + 1) * HALF], lhsT=x_codes[:, places].bitcast(FP8X4), lhsT_scale=x_scale[:, places], rhs=w1_codes[1][:].bitcast(FP8X4), rhs_scale=w1_scale[1][:], start=True, stop=True)
+                nc.tensor.matmul_mx(out=bank[:, c * HALF : (c + 1) * HALF], lhsT=x_codes[:, places].bitcast(FP8X4), lhsT_scale=x_scale[:, places], rhs=w1_codes[2][:].bitcast(FP8X4), rhs_scale=w1_scale[2][:], start=True, stop=True)
             gate = keep.tile([P, N], F32, name=f"turned_gate{h}")
             nc.scalar.activation(gate[:], bank[:], ACT.Sigmoid)
             return gate
@@ -160,14 +171,9 @@ def tile_picked_phcell_none_po_kernel(tc, x_words, x_scales, w1, w2, st, offs, o
         y_bf = [keep.tile([P, PACK * HALF], BF16, name=f"y_bf{h}", align_bytes=64) for h in range(2)]
         y = [keep.tile([P, PACK, HALF], F32, name=f"y{h}")[:] for h in range(2)]
 
-        def finish(engine, h, tiles, step):
-            engine.tensor_tensor(y[h][:, tiles, :], state_t[:, tiles, halves[h]], step, ALU.subtract)
+        def finish(engine, h, tiles, state, step):
+            engine.tensor_tensor(y[h][:, tiles, :], state, step, ALU.subtract)
             nc.sync.dma_start(out=out_rows[:, tiles, halves[h]], in_=y[h][:, tiles, :])
-
-        def direct_step(h):
-            step = keep.tile([P, 2, HALF], F32, name=f"step{h}", tag=("step0", "turned_step0")[h])
-            nc.vector.scalar_tensor_tensor(step[:], sums[:, h], -1.0, gates[h][:], ALU.add, ALU.mult)
-            return step
 
         def turned_step(h):
             step = keep.tile([P, N], F32, name=f"turned_step{h}")
@@ -181,14 +187,21 @@ def tile_picked_phcell_none_po_kernel(tc, x_words, x_scales, w1, w2, st, offs, o
         def rounding(h):
             return y_bf[h][:].rearrange("p (c i t) -> p c t i", i=4, t=PACK), y[h].rearrange("p t (c i) -> p c t i", i=4)
 
-        finish(nc.gpsimd, 0, PAIRS[0], direct_step(0)[:])
+        first_step = keep.tile([P, 2, HALF], F32, name="first_step")
+        for t in range(2):
+            nc.vector.scalar_tensor_tensor(first_step[:, t], first_sum[:, t], -1.0, gates[0][:, t], ALU.add, ALU.mult)
+        finish(nc.gpsimd, 0, PAIRS[0], st_first[:, :, :HALF], first_step[:])
+        last_sum.append(keep.tile([P, 2, CHUNK], F32, name="last_sum1", tag="first_step"))
+        nc.gpsimd.tensor_tensor(last_sum[1][:], st_quarter[1], n_direct[:, :, CHUNK:], ALU.add)
         backs = [turned_step(h) for h in range(2)]
-        finish(nc.vector, 0, PAIRS[1], backs[0][:])
-        last_step = direct_step(1)
-        finish(nc.vector, 1, PAIRS[1], backs[1][:])
-        for c in range(2):
-            part = slice(c * CHUNK, (c + 1) * CHUNK)
-            nc.vector.tensor_tensor(y[1][:, PAIRS[0], part], state_t[:, PAIRS[0], halves[1]][:, :, part], last_step[:, :, part], ALU.subtract)
+        for h in range(2):
+            finish(nc.vector, h, PAIRS[1], st_turn[:, :, halves[h]], backs[h][:])
+        last_step = keep.tile([P, 2, HALF], F32, name="last_step", tag="turned_step1")
+        parts = [slice(c * CHUNK, (c + 1) * CHUNK) for c in range(2)]
+        for c, part in enumerate(parts):
+            nc.vector.tensor_tensor(last_step[:, :, part], last_sum[c][:], gates[1][:, :, part], ALU.mult)
+        for c, part in enumerate(parts):
+            nc.vector.tensor_tensor(y[1][:, PAIRS[0], part], st_quarter[c], last_step[:, :, part], ALU.subtract)
         nc.sync.dma_start(out=out_rows[:, PAIRS[0], halves[1]], in_=y[1][:, PAIRS[0], :])
 
         def pack(lo, hi):

@@ -46,18 +46,18 @@ def tile_picked_phcell_none_po_kernel(tc, x_words, x_scales, w1, w2, st, offs, o
         word_table = shared.tile([P, T], U32, name="word_table", offset=0, align_bytes=64)
         nc.sync.dma_start(out=word_table[:].bitcast(I32), in_=x_words[0].rearrange("p c r -> p (c r)").bitcast(I32))
         x_scale = keep.tile([P, S], U8, name="x_scale", align_bytes=64)
-        nc.vector.memset(x_scale[:].bitcast(I32), 0)
         identity = keep.tile([P, P], F32, name="identity")
         nc.vector.memset(identity[:], 0.0)
         make_identity(nc, identity[:], nomemset=True)
 
         picked_scales = keep.tile([P, S], U8, name="picked_scales", align_bytes=64)
         nc.vector.tensor_copy(picked_scales[:], scale_table[:].indirect(offsets[:]))
+        nc.vector.tensor_copy(x_scale[:].bitcast(I32), picked_scales[:].bitcast(I32))
         w1_tile = keep.tile([P, PACK * N], F32, name="w1_tile", tag="w1_room", align_bytes=64)
         w1_raw = w1_tile[:]
         w1_rows = w1.rearrange("(p j) c -> p (j c)", j=PACK)
         nc.sync.dma_start(out=w1_raw[:, :N], in_=w1_rows[:, :N])
-        for i in range(4):
+        for i in range(1, 4):
             nc.sync.dma_start(out=x_scale[i:P:32, :].bitcast(I32), in_=picked_scales[8 * i : P : 32, :].bitcast(I32))
         for cols in (slice(N, 2 * N), slice(2 * N, 4 * N)):
             nc.sync.dma_start(out=w1_raw[:, cols], in_=w1_rows[:, cols])

@@ -59,7 +59,7 @@ def tile_picked_phcell_none_po_kernel(tc, x_words, x_scales, w1, w2, st, offs, o
         nc.sync.dma_start(out=w1_raw[:, :N], in_=w1_rows[:, :N])
         for i in range(1, 4):
             nc.sync.dma_start(out=x_scale[i:P:32, :].bitcast(I32), in_=picked_scales[8 * i : P : 32, :].bitcast(I32))
-        for cols in (slice(N, 2 * N), slice(2 * N, 4 * N)):
+        for cols in (slice(N, 4 * N),):
             nc.sync.dma_start(out=w1_raw[:, cols], in_=w1_rows[:, cols])
 
         def dealt(rounded, raw):
@@ -87,9 +87,8 @@ def tile_picked_phcell_none_po_kernel(tc, x_words, x_scales, w1, w2, st, offs, o
         dst = [w1_bf[u][:].rearrange("p (t m j) -> p m j t", t=2, j=PACK) for u in range(2)]
         w1_codes = [keep.tile([P, width], U32, name=f"w1_codes{u}", align_bytes=64) for u, width in enumerate((P, P, HALF))]
         w1_scale = [keep.tile([P, width], U8, name=f"w1_scale{u}", align_bytes=64) for u, width in enumerate((P, P, HALF))]
-        for rows in PAIRS:
-            for u in range(2):
-                nc.vector.tensor_copy(dst[u][:, :, rows], src[:, :, rows, PAIRS[u]])
+        for u in range(2):
+            nc.vector.tensor_copy(dst[u], src[:, :, :, PAIRS[u]])
         for u, rounded in enumerate((w1_bf[0][:, : PACK * P], w1_bf[0][:, PACK * P :], w1_bf[1][:])):
             nc.vector.quantize_mx(out=w1_codes[u][:].bitcast(FP8X4), scales=w1_scale[u][:], in_=rounded)
 

@@ -71,8 +71,9 @@ def tile_picked_phcell_none_po_kernel(tc, x_words, x_scales, w1, w2, st, offs, o
         st_first = room.tile([P, 2, S - CHUNK], F32, name="st_first", offset=0, align_bytes=64)
         st_last = room.tile([P, 2, CHUNK], F32, name="st_last", offset=8 * (S - CHUNK), align_bytes=64)
         st_turn = room.tile([P, 2, S], F32, name="st_turn", offset=8 * S, align_bytes=64)
+        nc.sync.dma_start(out=st_turn[:, :, :HALF], in_=st_rows[:, PAIRS[1], :HALF])
         nc.sync.dma_start(out=st_first[:], in_=st_rows[:, PAIRS[0], : S - CHUNK])
-        nc.sync.dma_start(out=st_turn[:], in_=st_rows[:, PAIRS[1], :])
+        nc.sync.dma_start(out=st_turn[:, :, HALF:], in_=st_rows[:, PAIRS[1], HALF:])
         nc.sync.dma_start(out=st_last[:], in_=st_rows[:, PAIRS[0], S - CHUNK :])
         st_quarter = (st_first[:, :, HALF:], st_last[:])
 
@@ -113,19 +114,21 @@ def tile_picked_phcell_none_po_kernel(tc, x_words, x_scales, w1, w2, st, offs, o
         turned_sum = [psum.tile([P, N], F32, name=f"turned_sum{h}", tag=f"new_bank1{h}") for h in range(2)]
         blocks = [(c, i) for c in range(2) for i in range(2)]
 
-        late_identity = shared.tile([P, P], F32, name="late_identity", offset=0, align_bytes=64)
+
+        late_identity = shared.tile([P, P], F32, name="late_identity", offset=4 * S, align_bytes=64)
         nc.scalar.copy(late_identity[:], identity[:])
 
         def turn_new(h):
             for b, (c, i) in enumerate(blocks):
-                nc.tensor.matmul(turned_sum[h][:, b * P : (b + 1) * P], lhsT=n_turn[h][:, i, c * P : (c + 1) * P], rhs=(identity, late_identity)[h][:], is_transpose=True, start=(b == 0), stop=False)
+                nc.tensor.matmul(turned_sum[h][:, b * P : (b + 1) * P], lhsT=n_turn[h][:, i, c * P : (c + 1) * P], rhs=identity[:], is_transpose=True, start=(b == 0), stop=False)
 
         def turn_state(h):
             for b, (c, i) in enumerate(blocks):
                 at = h * HALF + c * P
-                nc.tensor.matmul(turned_sum[h][:, b * P : (b + 1) * P], lhsT=st_turn[:, i, at : at + P], rhs=late_identity[:], is_transpose=True, start=False, stop=(b == 3))
+                nc.tensor.matmul(turned_sum[h][:, b * P : (b + 1) * P], lhsT=st_turn[:, i, at : at + P], rhs=(identity, late_identity)[h][:], is_transpose=True, start=False, stop=(b == 3))
 
         turn_new(0)
+        turn_new(1)
 
         first_sum = keep.tile([P, 2, HALF], F32, name="first_sum")
         nc.vector.scalar_tensor_tensor(first_sum[:], s_first[:], 2.0, st_first[:, :, :HALF], ALU.mult, ALU.add)
@@ -159,7 +162,6 @@ def tile_picked_phcell_none_po_kernel(tc, x_words, x_scales, w1, w2, st, offs, o
         gates = [direct_gate(0)]
         turned_gates = [turned_gate(h) for h in range(2)]
         turn_state(0)
-        turn_new(1)
         turn_state(1)
         gates.append(direct_gate(1))
 

@@ -138,7 +138,7 @@ def tile_picked_phcell_none_po_kernel(tc, x_words, x_scales, w1, w2, st, offs, o
         def direct_gate(h):
             gate = keep.tile([P, 2, HALF], F32, name=f"gate{h}")
             if h:
-                bank = psum.tile([P, 2, HALF], F32, name="last_gate_bank", tag="turned_bank0")
+                bank = psum.tile([P, 2, HALF], F32, name="last_gate_bank", tag="gate_bank1")
                 banks = [bank[:, t, :] for t in range(2)]
             else:
                 banks = [psum.tile([P, N], F32, name=f"gate_bank{t}")[:, :HALF] for t in range(2)]
@@ -150,13 +150,15 @@ def tile_picked_phcell_none_po_kernel(tc, x_words, x_scales, w1, w2, st, offs, o
                 nc.scalar.activation(gate[:], bank[:], ACT.Sigmoid)
             return gate
 
+        block_banks = [(f"turned_bank{h}", f"new_bank0{h}") for h in range(2)]
+
         def turned_gate(h):
-            bank = psum.tile([P, N], F32, name=f"turned_bank{h}")
-            for c in range(2):
-                places = slice(h * HALF + c * P, h * HALF + (c + 1) * P)
-                nc.tensor.matmul_mx(out=bank[:, c * HALF : (c + 1) * HALF], lhsT=x_codes[:, places].bitcast(FP8X4), lhsT_scale=x_scale[:, places], rhs=w1_codes[2][:].bitcast(FP8X4), rhs_scale=w1_scale[2][:], start=True, stop=True)
             gate = keep.tile([P, N], F32, name=f"turned_gate{h}")
-            nc.scalar.activation(gate[:], bank[:], ACT.Sigmoid)
+            for c in range(2):
+                bank = psum.tile([P, N], F32, name=f"turned_bank{h}{c}", tag=block_banks[h][c])
+                places = slice(h * HALF + c * P, h * HALF + (c + 1) * P)
+                nc.tensor.matmul_mx(out=bank[:, :HALF], lhsT=x_codes[:, places].bitcast(FP8X4), lhsT_scale=x_scale[:, places], rhs=w1_codes[2][:].bitcast(FP8X4), rhs_scale=w1_scale[2][:], start=True, stop=True)
+                nc.scalar.activation(gate[:, halves[c]], bank[:, :HALF], ACT.Sigmoid)
             return gate
 
         gates = [direct_gate(0)]
@@ -180,9 +182,9 @@ def tile_picked_phcell_none_po_kernel(tc, x_words, x_scales, w1, w2, st, offs, o
             step = keep.tile([P, N], F32, name=f"turned_step{h}")
             for half in halves:
                 nc.vector.tensor_tensor(step[:, half], turned_gates[h][:, half], turned_sum[h][:, half], ALU.mult)
-            back = psum.tile([P, 2, HALF], F32, name=f"back{h}", tag=f"new_bank0{h}")
+            back = [psum.tile([P, 2, HALF], F32, name=f"back{h}{c}", tag=block_banks[h][c])[:, :, :P] for c in range(2)]
             for b, (c, i) in enumerate(blocks):
-                nc.tensor.transpose(back[:, i, c * P : (c + 1) * P], step[:, b * P : (b + 1) * P], identity[:])
+                nc.tensor.transpose(back[c][:, i, :], step[:, b * P : (b + 1) * P], identity[:])
             return back
 
         def rounding(h):
@@ -192,11 +194,13 @@ def tile_picked_phcell_none_po_kernel(tc, x_words, x_scales, w1, w2, st, offs, o
         for t in range(2):
             nc.vector.scalar_tensor_tensor(first_step[:, t], first_sum[:, t], -1.0, gates[0][:, t], ALU.add, ALU.mult)
         finish(nc.gpsimd, 0, PAIRS[0], st_first[:, :, :HALF], first_step[:])
-        last_sum.append(keep.tile([P, 2, CHUNK], F32, name="last_sum1", tag="first_step"))
+        last_sum.append(keep.tile([P, 2, CHUNK], F32, name="last_sum1", tag="first_sum"))
         nc.gpsimd.tensor_tensor(last_sum[1][:], st_quarter[1], n_direct[:, :, CHUNK:], ALU.add)
         backs = [turned_step(h) for h in range(2)]
         for h in range(2):
-            finish(nc.vector, h, PAIRS[1], st_turn[:, :, halves[h]], backs[h][:])
+            for c in range(2):
+                nc.vector.tensor_tensor(y[h][:, PAIRS[1], c * P : (c + 1) * P], st_turn[:, :, h * HALF + c * P : h * HALF + (c + 1) * P], backs[h][c], ALU.subtract)
+            nc.sync.dma_start(out=out_rows[:, PAIRS[1], halves[h]], in_=y[h][:, PAIRS[1], :])
         last_step = keep.tile([P, 2, HALF], F32, name="last_step", tag="turned_step1")
         parts = [slice(c * CHUNK, (c + 1) * CHUNK) for c in range(2)]
         for c, part in enumerate(parts):

@@ -66,16 +66,18 @@ def tile_picked_phcell_none_po_kernel(tc, x_words, x_scales, w1, w2, st, offs, o
             return rounded[:].rearrange("p (t m j) -> p m j t", t=PACK, j=PACK), raw.rearrange("p (j m t) -> p m j t", j=PACK, t=PACK)
 
         w2_bf = keep.tile([P, PACK * N], BF16, name="w2_bf", tag="picked_room", align_bytes=64)
-        nc.vector.tensor_copy(*dealt(w2_bf, w2_raw[:]))
+        w2_dst, w2_src = dealt(w2_bf, w2_raw[:])
+        for tiles in PAIRS:
+            nc.vector.tensor_copy(w2_dst[:, :, :, tiles], w2_src[:, :, :, tiles])
         st_rows = st.rearrange("(p t) j -> p t j", t=PACK)
-        st_first = room.tile([P, 2, S - CHUNK], F32, name="st_first", offset=0, align_bytes=64)
-        st_last = room.tile([P, 2, CHUNK], F32, name="st_last", offset=8 * (S - CHUNK), align_bytes=64)
+        st_first = room.tile([P, 2, HALF], F32, name="st_first", offset=0, align_bytes=64)
+        st_last = room.tile([P, 2, HALF], F32, name="st_last", offset=8 * HALF, align_bytes=64)
         st_turn = room.tile([P, 2, S], F32, name="st_turn", offset=8 * S, align_bytes=64)
         nc.sync.dma_start(out=st_turn[:, :, :HALF], in_=st_rows[:, PAIRS[1], :HALF])
-        nc.sync.dma_start(out=st_first[:], in_=st_rows[:, PAIRS[0], : S - CHUNK])
+        nc.sync.dma_start(out=st_first[:], in_=st_rows[:, PAIRS[0], :HALF])
         nc.sync.dma_start(out=st_turn[:, :, HALF:], in_=st_rows[:, PAIRS[1], HALF:])
-        nc.sync.dma_start(out=st_last[:], in_=st_rows[:, PAIRS[0], S - CHUNK :])
-        st_quarter = (st_first[:, :, HALF:], st_last[:])
+        nc.sync.dma_start(out=st_last[:], in_=st_rows[:, PAIRS[0], HALF:])
+        st_quarter = (st_last[:, :, :CHUNK], st_last[:, :, CHUNK:])
 
         w2_codes = keep.tile([P, N], U32, name="w2_codes", align_bytes=64)
         w2_scale = keep.tile([P, N], U8, name="w2_scale", align_bytes=64)
@@ -132,8 +134,6 @@ def tile_picked_phcell_none_po_kernel(tc, x_words, x_scales, w1, w2, st, offs, o
 
         first_sum = keep.tile([P, 2, HALF], F32, name="first_sum")
         nc.vector.scalar_tensor_tensor(first_sum[:], s_first[:], 2.0, st_first[:, :, :HALF], ALU.mult, ALU.add)
-        last_sum = [keep.tile([P, 2, CHUNK], F32, name="last_sum0")]
-        nc.vector.tensor_tensor(last_sum[0][:], st_quarter[0], n_direct[:, :, :CHUNK], ALU.add)
 
         def direct_gate(h):
             gate = keep.tile([P, 2, HALF], F32, name=f"gate{h}")
@@ -174,10 +174,6 @@ def tile_picked_phcell_none_po_kernel(tc, x_words, x_scales, w1, w2, st, offs, o
         y_bf = [keep.tile([P, PACK * HALF], BF16, name=f"y_bf{h}", align_bytes=64) for h in range(2)]
         y = [keep.tile([P, PACK, HALF], F32, name=f"y{h}")[:] for h in range(2)]
 
-        def finish(engine, h, tiles, state, step):
-            engine.tensor_tensor(y[h][:, tiles, :], state, step, ALU.subtract)
-            nc.sync.dma_start(out=out_rows[:, tiles, halves[h]], in_=y[h][:, tiles, :])
-
         def turned_step(h):
             step = keep.tile([P, N], F32, name=f"turned_step{h}")
             for half in halves:
@@ -193,9 +189,11 @@ def tile_picked_phcell_none_po_kernel(tc, x_words, x_scales, w1, w2, st, offs, o
         first_step = keep.tile([P, 2, HALF], F32, name="first_step")
         for t in range(2):
             nc.vector.scalar_tensor_tensor(first_step[:, t], first_sum[:, t], -1.0, gates[0][:, t], ALU.add, ALU.mult)
-        finish(nc.gpsimd, 0, PAIRS[0], st_first[:, :, :HALF], first_step[:])
-        last_sum.append(keep.tile([P, 2, CHUNK], F32, name="last_sum1", tag="first_sum"))
-        nc.gpsimd.tensor_tensor(last_sum[1][:], st_quarter[1], n_direct[:, :, CHUNK:], ALU.add)
+        for t, engine in enumerate((nc.vector, nc.gpsimd)):
+            engine.tensor_tensor(y[0][:, t], st_first[:, t], first_step[:, t], ALU.subtract)
+        nc.sync.dma_start(out=out_rows[:, PAIRS[0], halves[0]], in_=y[0][:, PAIRS[0], :])
+        last_sum = keep.tile([P, 2, HALF], F32, name="last_sum", tag="first_sum")
+        nc.gpsimd.tensor_tensor(last_sum[:], st_last[:], n_direct[:], ALU.add)
         backs = [turned_step(h) for h in range(2)]
         for h in range(2):
             for c in range(2):
@@ -204,7 +202,7 @@ def tile_picked_phcell_none_po_kernel(tc, x_words, x_scales, w1, w2, st, offs, o
         last_step = keep.tile([P, 2, HALF], F32, name="last_step", tag="turned_step1")
         parts = [slice(c * CHUNK, (c + 1) * CHUNK) for c in range(2)]
         for c, part in enumerate(parts):
-            nc.vector.tensor_tensor(last_step[:, :, part], last_sum[c][:], gates[1][:, :, part], ALU.mult)
+            nc.vector.tensor_tensor(last_step[:, :, part], last_sum[:, :, part], gates[1][:, :, part], ALU.mult)
         for c, part in enumerate(parts):
             nc.vector.tensor_tensor(y[1][:, PAIRS[0], part], st_quarter[c], last_step[:, :, part], ALU.subtract)
         nc.sync.dma_start(out=out_rows[:, PAIRS[0], halves[1]], in_=y[1][:, PAIRS[0], :])

@@ -22,6 +22,7 @@ HALF = S // 2
 CHUNK = 128
 PAIRS = (slice(0, 2), slice(2, 4))
 LEAD = (slice(0, 768),)
+SPLIT = 80
 
 
 def tile_picked_phcell_none_po_kernel(tc, x_words, x_scales, w1, w2, st, offs, out_0, out_1, out_2):
@@ -90,10 +91,6 @@ def tile_picked_phcell_none_po_kernel(tc, x_words, x_scales, w1, w2, st, offs, o
         dst = [w1_bf[u][:].rearrange("p (t m j) -> p m j t", t=2, j=PACK) for u in range(2)]
         w1_codes = [keep.tile([P, width], U32, name=f"w1_codes{u}", align_bytes=64) for u, width in enumerate((P, P, HALF))]
         w1_scale = [keep.tile([P, width], U8, name=f"w1_scale{u}", align_bytes=64) for u, width in enumerate((P, P, HALF))]
-        for u in range(2):
-            nc.vector.tensor_copy(dst[u], src[:, :, :, PAIRS[u]])
-        for u, rounded in enumerate((w1_bf[0][:, : PACK * P], w1_bf[0][:, PACK * P :], w1_bf[1][:])):
-            nc.vector.quantize_mx(out=w1_codes[u][:].bitcast(FP8X4), scales=w1_scale[u][:], in_=rounded)
 
         halves = [slice(h * HALF, (h + 1) * HALF) for h in range(2)]
 
@@ -105,20 +102,23 @@ def tile_picked_phcell_none_po_kernel(tc, x_words, x_scales, w1, w2, st, offs, o
             nc.scalar.activation(result, bank, func, scale=scale)
 
         s_first = keep.tile([P, 2, HALF], F32, name="s_first")
-        n_direct = keep.tile([P, 2, HALF], F32, name="n_direct")
         n_tile = keep.tile([P, 2, 2, HALF], F32, name="n_tile")
         n_turn = (n_tile[:, 0], n_tile[:, 1])
         new_of(0, halves[0], "new_bank00", s_first[:], ACT.Sigmoid, -2.0)
         for h in range(2):
             new_of(1, halves[h], f"new_bank1{h}", n_turn[h], ACT.Tanh, -1.0)
+        nc.vector.tensor_copy(dst[0], src[:, :, :, PAIRS[0]])
+        nc.vector.tensor_copy(dst[1][:, :SPLIT], src[:, :SPLIT, :, PAIRS[1]])
+        nc.scalar.activation(dst[1][:, SPLIT:], src[:, SPLIT:, :, PAIRS[1]], ACT.Copy)
+        for u, rounded in enumerate((w1_bf[0][:, : PACK * P], w1_bf[0][:, PACK * P :], w1_bf[1][:])):
+            nc.vector.quantize_mx(out=w1_codes[u][:].bitcast(FP8X4), scales=w1_scale[u][:], in_=rounded)
+        n_direct = keep.tile([P, 2, HALF], F32, name="n_direct")
         new_of(0, halves[1], "new_bank01", n_direct[:], ACT.Tanh, -1.0)
 
         turned_sum = [psum.tile([P, N], F32, name=f"turned_sum{h}", tag=f"new_bank1{h}") for h in range(2)]
         blocks = [(c, i) for c in range(2) for i in range(2)]
 
-
         late_identity = shared.tile([P, P], F32, name="late_identity", offset=4 * S, align_bytes=64)
-        nc.scalar.copy(late_identity[:], identity[:])
 
         def turn_new(h):
             for b, (c, i) in enumerate(blocks):
@@ -134,6 +134,7 @@ def tile_picked_phcell_none_po_kernel(tc, x_words, x_scales, w1, w2, st, offs, o
 
         first_sum = keep.tile([P, 2, HALF], F32, name="first_sum")
         nc.vector.scalar_tensor_tensor(first_sum[:], s_first[:], 2.0, st_first[:, :, :HALF], ALU.mult, ALU.add)
+        nc.vector.tensor_copy(late_identity[:], identity[:])
 
         def direct_gate(h):
             gate = keep.tile([P, 2, HALF], F32, name=f"gate{h}")

@@ -118,7 +118,6 @@ def tile_picked_phcell_none_po_kernel(tc, x_words, x_scales, w1, w2, st, offs, o
         turned_sum = [psum.tile([P, N], F32, name=f"turned_sum{h}", tag=f"new_bank1{h}") for h in range(2)]
         blocks = [(c, i) for c in range(2) for i in range(2)]
 
-        late_identity = shared.tile([P, P], F32, name="late_identity", offset=4 * S, align_bytes=64)
 
         def turn_new(h):
             for b, (c, i) in enumerate(blocks):
@@ -127,14 +126,13 @@ def tile_picked_phcell_none_po_kernel(tc, x_words, x_scales, w1, w2, st, offs, o
         def turn_state(h):
             for b, (c, i) in enumerate(blocks):
                 at = h * HALF + c * P
-                nc.tensor.matmul(turned_sum[h][:, b * P : (b + 1) * P], lhsT=st_turn[:, i, at : at + P], rhs=(identity, late_identity)[h][:], is_transpose=True, start=False, stop=(b == 3))
+                nc.tensor.matmul(turned_sum[h][:, b * P : (b + 1) * P], lhsT=st_turn[:, i, at : at + P], rhs=identity[:], is_transpose=True, start=False, stop=(b == 3))
 
         turn_new(0)
         turn_new(1)
 
         first_sum = keep.tile([P, 2, HALF], F32, name="first_sum")
         nc.vector.scalar_tensor_tensor(first_sum[:], s_first[:], 2.0, st_first[:, :, :HALF], ALU.mult, ALU.add)
-        nc.vector.tensor_copy(late_identity[:], identity[:])
 
         def direct_gate(h):
             gate = keep.tile([P, 2, HALF], F32, name=f"gate{h}")

from contextlib import ExitStack

import concourse.mybir as mybir
from concourse.masks import make_identity

K, T, S, N = 512, 2048, 512, 512
FLOPS = 2 * 2 * K * N * S

F32 = mybir.dt.float32
BF16 = mybir.dt.bfloat16
I32 = mybir.dt.int32
U32 = mybir.dt.uint32
U16 = mybir.dt.uint16
U8 = mybir.dt.uint8
FP8X4 = mybir.dt.float8_e4m3fn_x4
ACT = mybir.ActivationFunctionType
ALU = mybir.AluOpType

P = 128
PACK = 4
HALF = S // 2
CHUNK = 128
PAIRS = (slice(0, 2), slice(2, 4))
LEAD = (slice(0, 768),)
SPLIT = 80


def tile_picked_phcell_none_po_kernel(tc, x_words, x_scales, w1, w2, st, offs, out_0, out_1, out_2):
    nc = tc.nc
    with ExitStack() as ctx:
        keep = ctx.enter_context(tc.tile_pool(name="keep", bufs=1))
        shared = ctx.enter_context(tc.tile_pool(name="shared", bufs=1))
        room = ctx.enter_context(tc.tile_pool(name="room", bufs=1))
        psum = ctx.enter_context(tc.psum_pool(name="psum", bufs=1))


        scale_table = keep.tile([P, T], U8, name="scale_table", tag="w1_room", align_bytes=64)
        nc.vector.memset(scale_table[:].bitcast(I32), 0)
        w2_raw = room.tile([P, PACK * N], F32, name="w2_raw", offset=0, align_bytes=64)
        w2_rows = w2.rearrange("(p j) c -> p (j c)", j=PACK)
        for cols in LEAD:
            nc.sync.dma_start(out=w2_raw[:, cols], in_=w2_rows[:, cols])
        offsets = keep.tile([P, S // 16], U16, name="offsets")
        nc.sync.dma_start(offsets[:], offs)
        nc.sync.dma_start(out=scale_table[0:P:8, :].bitcast(I32), in_=x_scales[0].bitcast(I32))
        nc.sync.dma_start(out=w2_raw[:, LEAD[-1].stop :], in_=w2_rows[:, LEAD[-1].stop :])
        word_table = shared.tile([P, T], U32, name="word_table", offset=0, align_bytes=64)
        nc.sync.dma_start(out=word_table[:].bitcast(I32), in_=x_words[0].rearrange("p c r -> p (c r)").bitcast(I32))
        x_scale = keep.tile([P, S], U8, name="x_scale", align_bytes=64)
        identity = keep.tile([P, P], F32, name="identity")
        nc.vector.memset(identity[:], 0.0)
        make_identity(nc, identity[:], nomemset=True)

        picked_scales = keep.tile([P, S], U8, name="picked_scales", align_bytes=64)
        nc.vector.tensor_copy(picked_scales[:], scale_table[:].indirect(offsets[:]))
        nc.vector.tensor_copy(x_scale[:].bitcast(I32), picked_scales[:].bitcast(I32))
        w1_tile = keep.tile([P, PACK * N], F32, name="w1_tile", tag="w1_room", align_bytes=64)
        w1_raw = w1_tile[:]
        w1_rows = w1.rearrange("(p j) c -> p (j c)", j=PACK)
        nc.sync.dma_start(out=w1_raw[:, :N], in_=w1_rows[:, :N])
        for i in range(1, 4):
            nc.sync.dma_start(out=x_scale[i:P:32, :].bitcast(I32), in_=picked_scales[8 * i : P : 32, :].bitcast(I32))
        for cols in (slice(N, 4 * N),):
            nc.sync.dma_start(out=w1_raw[:, cols], in_=w1_rows[:, cols])

        def dealt(rounded, raw):
            return rounded[:].rearrange("p (t m j) -> p m j t", t=PACK, j=PACK), raw.rearrange("p (j m t) -> p m j t", j=PACK, t=PACK)

        w2_bf = keep.tile([P, PACK * N], BF16, name="w2_bf", tag="picked_room", align_bytes=64)
        w2_dst, w2_src = dealt(w2_bf, w2_raw[:])
        for tiles in PAIRS:
            nc.vector.tensor_copy(w2_dst[:, :, :, tiles], w2_src[:, :, :, tiles])
        st_rows = st.rearrange("(p t) j -> p t j", t=PACK)
        st_first = room.tile([P, 2, HALF], F32, name="st_first", offset=0, align_bytes=64)
        st_last = room.tile([P, 2, HALF], F32, name="st_last", offset=8 * HALF, align_bytes=64)
        st_turn = room.tile([P, 2, S], F32, name="st_turn", offset=8 * S, align_bytes=64)
        nc.sync.dma_start(out=st_turn[:, :, :HALF], in_=st_rows[:, PAIRS[1], :HALF])
        nc.sync.dma_start(out=st_first[:], in_=st_rows[:, PAIRS[0], :HALF])
        nc.sync.dma_start(out=st_turn[:, :, HALF:], in_=st_rows[:, PAIRS[1], HALF:])
        nc.sync.dma_start(out=st_last[:], in_=st_rows[:, PAIRS[0], HALF:])
        st_quarter = (st_last[:, :, :CHUNK], st_last[:, :, CHUNK:])

        w2_codes = keep.tile([P, N], U32, name="w2_codes", align_bytes=64)
        w2_scale = keep.tile([P, N], U8, name="w2_scale", align_bytes=64)
        nc.vector.quantize_mx(out=w2_codes[:].bitcast(FP8X4), scales=w2_scale[:], in_=w2_bf[:])
        x_codes = keep.tile([P, S], U32, name="x_codes", tag="picked_room", align_bytes=64)
        for h in range(2):
            nc.vector.tensor_copy(x_codes[:, h * HALF : (h + 1) * HALF], word_table[:].indirect(offsets[:, h * HALF // 16 : (h + 1) * HALF // 16]))
        w1_bf = [shared.tile([P, PACK * HALF], BF16, name=f"w1_bf{u}", offset=u * 4 * S, align_bytes=64) for u in range(2)]
        src = w1_raw.rearrange("p (j m t) -> p m j t", j=PACK, t=PACK)
        dst = [w1_bf[u][:].rearrange("p (t m j) -> p m j t", t=2, j=PACK) for u in range(2)]
        w1_codes = [keep.tile([P, width], U32, name=f"w1_codes{u}", align_bytes=64) for u, width in enumerate((P, P, HALF))]
        w1_scale = [keep.tile([P, width], U8, name=f"w1_scale{u}", align_bytes=64) for u, width in enumerate((P, P, HALF))]

        halves = [slice(h * HALF, (h + 1) * HALF) for h in range(2)]

        def new_of(u, places, tag, result, func, scale):
            bank = psum.tile([P, 2, HALF], F32, name=f"new_{tag}", tag=tag)[:, :, : places.stop - places.start]
            for i in range(2):
                cols = slice((2 * u + i) * P, (2 * u + i + 1) * P)
                nc.tensor.matmul_mx(out=bank[:, i, :], lhsT=w2_codes[:, cols].bitcast(FP8X4), lhsT_scale=w2_scale[:, cols], rhs=x_codes[:, places].bitcast(FP8X4), rhs_scale=x_scale[:, places], start=True, stop=True)
            nc.scalar.activation(result, bank, func, scale=scale)

        s_first = keep.tile([P, 2, HALF], F32, name="s_first")
        n_tile = keep.tile([P, 2, 2, HALF], F32, name="n_tile")
        n_turn = (n_tile[:, 0], n_tile[:, 1])
        new_of(0, halves[0], "new_bank00", s_first[:], ACT.Sigmoid, -2.0)
        for h in range(2):
            new_of(1, halves[h], f"new_bank1{h}", n_turn[h], ACT.Tanh, -1.0)
        nc.vector.tensor_copy(dst[0], src[:, :, :, PAIRS[0]])
        nc.vector.tensor_copy(dst[1][:, :SPLIT], src[:, :SPLIT, :, PAIRS[1]])
        nc.scalar.activation(dst[1][:, SPLIT:], src[:, SPLIT:, :, PAIRS[1]], ACT.Copy)
        for u, rounded in enumerate((w1_bf[0][:, : PACK * P], w1_bf[0][:, PACK * P :], w1_bf[1][:])):
            nc.vector.quantize_mx(out=w1_codes[u][:].bitcast(FP8X4), scales=w1_scale[u][:], in_=rounded)
        n_direct = keep.tile([P, 2, HALF], F32, name="n_direct")
        new_of(0, halves[1], "new_bank01", n_direct[:], ACT.Tanh, -1.0)

        turned_sum = [psum.tile([P, N], F32, name=f"turned_sum{h}", tag=f"new_bank1{h}") for h in range(2)]
        blocks = [(c, i) for c in range(2) for i in range(2)]


        def turn_new(h):
            for b, (c, i) in enumerate(blocks):
                nc.tensor.matmul(turned_sum[h][:, b * P : (b + 1) * P], lhsT=n_turn[h][:, i, c * P : (c + 1) * P], rhs=identity[:], is_transpose=True, start=(b == 0), stop=False)

        def turn_state(h):
            for b, (c, i) in enumerate(blocks):
                at = h * HALF + c * P
                nc.tensor.matmul(turned_sum[h][:, b * P : (b + 1) * P], lhsT=st_turn[:, i, at : at + P], rhs=identity[:], is_transpose=True, start=False, stop=(b == 3))

        turn_new(0)
        turn_new(1)

        first_sum = keep.tile([P, 2, HALF], F32, name="first_sum")
        nc.vector.scalar_tensor_tensor(first_sum[:], s_first[:], 2.0, st_first[:, :, :HALF], ALU.mult, ALU.add)

        def direct_gate(h):
            gate = keep.tile([P, 2, HALF], F32, name=f"gate{h}")
            if h:
                bank = psum.tile([P, 2, HALF], F32, name="last_gate_bank", tag="gate_bank1")
                banks = [bank[:, t, :] for t in range(2)]
            else:
                banks = [psum.tile([P, N], F32, name=f"gate_bank{t}")[:, :HALF] for t in range(2)]
            for t in range(2):
                nc.tensor.matmul_mx(out=banks[t], lhsT=w1_codes[t][:].bitcast(FP8X4), lhsT_scale=w1_scale[t][:], rhs=x_codes[:, halves[h]].bitcast(FP8X4), rhs_scale=x_scale[:, halves[h]], start=True, stop=True)
                if not h:
                    nc.scalar.activation(gate[:, t, :], banks[t], ACT.Sigmoid)
            if h:
                nc.scalar.activation(gate[:], bank[:], ACT.Sigmoid)
            return gate

        block_banks = [(f"turned_bank{h}", f"new_bank0{h}") for h in range(2)]

        def turned_gate(h):
            gate = keep.tile([P, N], F32, name=f"turned_gate{h}")
            for c in range(2):
                bank = psum.tile([P, N], F32, name=f"turned_bank{h}{c}", tag=block_banks[h][c])
                places = slice(h * HALF + c * P, h * HALF + (c + 1) * P)
                nc.tensor.matmul_mx(out=bank[:, :HALF], lhsT=x_codes[:, places].bitcast(FP8X4), lhsT_scale=x_scale[:, places], rhs=w1_codes[2][:].bitcast(FP8X4), rhs_scale=w1_scale[2][:], start=True, stop=True)
                nc.scalar.activation(gate[:, halves[c]], bank[:, :HALF], ACT.Sigmoid)
            return gate

        gates = [direct_gate(0)]
        turned_gates = [turned_gate(h) for h in range(2)]
        turn_state(0)
        turn_state(1)
        gates.append(direct_gate(1))

        out_rows = out_0.rearrange("(p t) j -> p t j", t=PACK)
        out_words = out_1[0].rearrange("p c r -> p (c r)").bitcast(I32)
        y_scale = keep.tile([P, S], U8, name="y_scale", align_bytes=64)
        y_codes = [keep.tile([P, HALF], U32, name=f"y_codes{h}", align_bytes=64) for h in range(2)]
        y_bf = [keep.tile([P, PACK * HALF], BF16, name=f"y_bf{h}", align_bytes=64) for h in range(2)]
        y = [keep.tile([P, PACK, HALF], F32, name=f"y{h}")[:] for h in range(2)]

        def turned_step(h):
            step = keep.tile([P, N], F32, name=f"turned_step{h}")
            for half in halves:
                nc.vector.tensor_tensor(step[:, half], turned_gates[h][:, half], turned_sum[h][:, half], ALU.mult)
            back = [psum.tile([P, 2, HALF], F32, name=f"back{h}{c}", tag=block_banks[h][c])[:, :, :P] for c in range(2)]
            for b, (c, i) in enumerate(blocks):
                nc.tensor.transpose(back[c][:, i, :], step[:, b * P : (b + 1) * P], identity[:])
            return back

        def rounding(h):
            return y_bf[h][:].rearrange("p (c i t) -> p c t i", i=4, t=PACK), y[h].rearrange("p t (c i) -> p c t i", i=4)

        first_step = keep.tile([P, 2, HALF], F32, name="first_step")
        for t in range(2):
            nc.vector.scalar_tensor_tensor(first_step[:, t], first_sum[:, t], -1.0, gates[0][:, t], ALU.add, ALU.mult)
        for t, engine in enumerate((nc.vector, nc.gpsimd)):
            engine.tensor_tensor(y[0][:, t], st_first[:, t], first_step[:, t], ALU.subtract)
        nc.sync.dma_start(out=out_rows[:, PAIRS[0], halves[0]], in_=y[0][:, PAIRS[0], :])
        last_sum = keep.tile([P, 2, HALF], F32, name="last_sum", tag="first_sum")
        nc.gpsimd.tensor_tensor(last_sum[:], st_last[:], n_direct[:], ALU.add)
        backs = [turned_step(h) for h in range(2)]
        for h in range(2):
            for c in range(2):
                nc.vector.tensor_tensor(y[h][:, PAIRS[1], c * P : (c + 1) * P], st_turn[:, :, h * HALF + c * P : h * HALF + (c + 1) * P], backs[h][c], ALU.subtract)
            nc.sync.dma_start(out=out_rows[:, PAIRS[1], halves[h]], in_=y[h][:, PAIRS[1], :])
        last_step = keep.tile([P, 2, HALF], F32, name="last_step", tag="turned_step1")
        parts = [slice(c * CHUNK, (c + 1) * CHUNK) for c in range(2)]
        for c, part in enumerate(parts):
            nc.vector.tensor_tensor(last_step[:, :, part], last_sum[:, :, part], gates[1][:, :, part], ALU.mult)
        for c, part in enumerate(parts):
            nc.vector.tensor_tensor(y[1][:, PAIRS[0], part], st_quarter[c], last_step[:, :, part], ALU.subtract)
        nc.sync.dma_start(out=out_rows[:, PAIRS[0], halves[1]], in_=y[1][:, PAIRS[0], :])

        def pack(lo, hi):
            h, at = divmod(lo, HALF)
            nc.vector.quantize_mx(out=y_codes[h][:, at : at + hi - lo].bitcast(FP8X4), scales=y_scale[:, lo:hi], in_=y_bf[h][:, PACK * at : PACK * (at + hi - lo)])

        nc.scalar.activation(*rounding(0), ACT.Copy)
        dst, src = rounding(1)
        nc.scalar.activation(dst[:, :32], src[:, :32], ACT.Copy)
        pack(0, HALF)
        nc.sync.dma_start(out=out_words[:, halves[0]], in_=y_codes[0][:].bitcast(I32))
        nc.vector.tensor_copy(dst[:, 32:], src[:, 32:])
        pack(HALF, HALF + CHUNK)
        pack(HALF + CHUNK, S)
        nc.sync.dma_start(out=out_words[:, halves[1]], in_=y_codes[1][:].bitcast(I32))
        for quad in range(4):
            queue = nc.scalar if quad % 2 else nc.sync
            queue.dma_start(out=out_2[0, 4 * quad : 4 * quad + 4, :].bitcast(I32), in_=y_scale[32 * quad : 32 * quad + 4, :].bitcast(I32))
